import numpy as np
import ml_dtypes


def mxq(x, axis, fmt="e4m3"):
    dtype, down = {"e4m3": (ml_dtypes.float8_e4m3fn, 7), "e5m2": (ml_dtypes.float8_e5m2, 14)}[fmt]
    v = np.moveaxis(np.asarray(x, np.float32).astype(ml_dtypes.bfloat16).astype(np.float64), axis, -1)
    blocks = v.reshape(v.shape[:-1] + (-1, 32))
    amax = np.abs(blocks).max(-1, keepdims=True)
    byte = np.maximum(np.where(amax > 0, np.frexp(amax)[1] - 1 + 127, 0) - down, 1)
    scale = np.exp2(byte - 127.0)
    codes = (blocks / scale).astype(np.float32).astype(dtype).astype(np.float64)
    return np.moveaxis((codes * scale).reshape(v.shape), -1, axis)


WIDE = False


def mx_kscale(k):
    if not WIDE:
        return np.ones(k)
    levels = np.array([10, -10, 5, -5, 0])
    if k % 512:
        return np.exp2(np.random.permutation(np.resize(levels, k // 32))).repeat(32)
    a = np.empty((k // 512, 16))
    for p in range(k // 512):
        a[p, :8] = np.random.permutation(np.resize(levels, 8))
        for g in range(8):
            far = levels[np.abs(levels - a[p, g]) >= 10]
            a[p, g + 8] = far[np.random.randint(len(far))]
    return np.exp2(a.ravel()).repeat(32)


def f64(x):
    return np.asarray(x).astype(np.float64)


def striped(idx):
    return np.tile(idx.reshape(-1, 16).T, (8, 1)).astype(np.uint16)


def unstriped(offs):
    return offs[:16].T.reshape(-1).astype(np.int64)


def pack_weight(w):
    k, n = w.shape
    w = f64(np.asarray(w, np.float32).astype(ml_dtypes.bfloat16)).reshape(k // 32, 32, n)
    amax = np.abs(w).max(1)
    byte = np.clip(np.where(amax > 0, np.frexp(amax)[1] - 1 + 127 - 7, 1), 1, 254)
    scaled = (w * np.exp2(127.0 - byte)[:, None, :]).reshape(k, n).astype(np.float32)
    words = np.ascontiguousarray(scaled.reshape(k // 512, 128, 4, n).transpose(0, 1, 3, 2)).astype(ml_dtypes.float8_e4m3fn).view(np.uint8)
    return words, np.ascontiguousarray(byte.astype(np.uint8).reshape(k // 512, 16, n))


def unpack_weight(words, scales):
    g, p, n, _ = words.shape
    vals = np.ascontiguousarray(words).view(ml_dtypes.float8_e4m3fn).astype(np.float64) * np.repeat(np.exp2(scales.astype(np.float64) - 127.0), 8, axis=1)[..., None]
    return vals.transpose(0, 1, 3, 2).reshape(g * 512, n)


K, T, S, D, V, N = 1024, 2048, 1024, 3, 512, 256
P = 2 ** 7


def setup_inputs():
    n = np.random.standard_normal
    s = mx_kscale(K)[:, None]
    packed_xT = pack_weight(n((K, T)) * s)
    return {
        "x_words": packed_xT[0],
        "x_scales": packed_xT[1],
        "w1": (n((K, N)) / np.sqrt(K) / s).astype(np.float32),
        "score": np.tile(np.random.standard_normal((D, 1, V)), (1, P, 1)).astype(np.float32),
        "offs": striped(np.random.permutation(T)[:S]),
        "pos1": striped(np.random.permutation(S)[:V]),
        "pos2": striped(np.random.permutation(S)[:V]),
        "pos3": striped(np.random.permutation(S)[:V]),
    }


def reference(x_words, x_scales, w1, score, offs, pos1, pos2, pos3):
    xq = unpack_weight(x_words, x_scales)[:, unstriped(offs)]
    y = mxq(f64(w1), 0, "e4m3").T @ xq
    e0 = np.exp(f64(score)[0, :1])
    e1 = np.exp(f64(score)[1, :1])
    e2 = np.exp(f64(score)[2, :1])
    num = y[:, unstriped(pos1)] * e0 + y[:, unstriped(pos2)] * e1 + y[:, unstriped(pos3)] * e2
    den = e0 + e1 + e2
    return num / den

@@ -1,0 +1,193 @@
+from contextlib import ExitStack
+
+import concourse.mybir as mybir
+from concourse.masks import make_identity
+
+K, T, S, D, V, N = 1024, 2048, 1024, 3, 512, 256
+FLOPS = 2 * K * N * S
+BYTES = K * T + K * T // 32 + K * N * 4 + D * V * 4 + 128 * (S + D * V) // 16 * 2 + N * V * 4
+
+F32 = mybir.dt.float32
+BF16 = mybir.dt.bfloat16
+I32 = mybir.dt.int32
+U32 = mybir.dt.uint32
+U16 = mybir.dt.uint16
+U8 = mybir.dt.uint8
+FP8X4 = mybir.dt.float8_e4m3fn_x4
+ALU = mybir.AluOpType
+ACT = mybir.ActivationFunctionType
+
+P = 128
+PACK = 4
+PASSES = K // (P * PACK)
+BLOCKS = N // P
+BANK = 512
+LAST = 256
+
+
+def tile_picked_gatv_none_p_kernel(
+    tc, x_words, x_scales, w1, score, offs, pos1, pos2, pos3, out
+):
+    nc = tc.nc
+    with ExitStack() as ctx:
+        lists = ctx.enter_context(tc.tile_pool(name="lists", bufs=1))
+        keep = ctx.enter_context(tc.tile_pool(name="keep", bufs=1))
+        psum = ctx.enter_context(tc.psum_pool(name="psum", bufs=1))
+
+        offs_t = lists.tile([P, S // 16], U16, name="offs_t")
+        pos_t = [lists.tile([P, V // 16], U16, name=f"pos_t{d}") for d in range(D)]
+
+        scale_win = keep.tile([P, T], U8, name="scale_win", align_bytes=64)
+        nc.vector.memset(scale_win[:].bitcast(I32), 0)
+
+        nc.sync.dma_start(offs_t[:], offs)
+        s_t = keep.tile([P, D, 8], F32, name="s_t")
+        nc.sync.dma_start(s_t[:, :, 0:4], score[:, 0, :].rearrange("d (p j) -> p d j", j=4))
+        word_win = [keep.tile([P, T], I32, name=f"word_win{z}", align_bytes=64) for z in range(PASSES)]
+        w_raw = {}
+
+        def load_words(z):
+            nc.sync.dma_start(word_win[z][:], x_words[z].rearrange("p c r -> p (c r)").bitcast(I32))
+
+        def load_weights(b):
+            for z in range(PASSES):
+                w_raw[b, z] = keep.tile([P, PACK, P], F32, name=f"w_raw{b}{z}")
+                nc.sync.dma_start(
+                    w_raw[b, z][:],
+                    w1[z * P * PACK : (z + 1) * P * PACK, b * P : (b + 1) * P].rearrange("(p j) c -> p j c", j=PACK),
+                )
+
+        load_words(0)
+        for q in range(4):
+            nc.sync.dma_start(
+                scale_win[32 * q : 32 * q + 8, :].bitcast(I32),
+                x_scales[:, 4 * q : 4 * q + 4, :].bitcast(I32),
+            )
+        load_weights(0)
+        load_words(1)
+        load_weights(1)
+        for d, pos in enumerate((pos1, pos2, pos3)):
+            nc.sync.dma_start(pos_t[d][:], pos)
+
+        ident = keep.tile([P, P], F32, name="ident")
+        make_identity(nc, ident[:])
+
+        warm = keep.tile([P, 1], F32, name="warm")
+        nc.gpsimd.memset(warm[:], 0.0)
+        warm_out = keep.tile([P, 1], F32, name="warm_out")
+        nc.scalar.activation(warm_out[:], warm[:], ACT.Exp)
+
+        s_max = keep.tile([P, 4], F32, name="s_max")
+        nc.vector.tensor_reduce(s_max[:], s_t[:, :, 0:4].rearrange("p d j -> p j d"), mybir.AxisListType.X, ALU.max)
+        shifted = keep.tile([P, D, 4], F32, name="shifted")
+        nc.vector.tensor_tensor(shifted[:], s_t[:, :, 0:4], s_max[:].unsqueeze(1).to_broadcast([P, D, 4]), ALU.subtract)
+        e_t = keep.tile([P, D, 4], F32, name="e_t")
+        nc.scalar.activation(e_t[:], shifted[:], ACT.Exp)
+        total = keep.tile([P, 4], F32, name="total")
+        nc.vector.tensor_reduce(total[:], e_t[:].rearrange("p d j -> p j d"), mybir.AxisListType.X, ALU.add)
+        inv = keep.tile([P, 4], F32, name="inv")
+        nc.vector.reciprocal(inv[:], total[:])
+        a_t = keep.tile([P, D, 4], F32, name="a_t")
+        nc.vector.tensor_tensor(a_t[:], e_t[:], inv[:].unsqueeze(1).to_broadcast([P, D, 4]), ALU.mult)
+        a_rows = []
+        for d in range(D):
+            bank = psum.tile([P, 4, P], F32, name=f"spread{d}", tag=f"t{d}")
+            for j in range(4):
+                nc.tensor.transpose(bank[:, j, :], a_t[:, d, j : j + 1].to_broadcast([P, P]), ident[:])
+            row = keep.tile([P, P, 4], F32, name=f"a_row{d}")
+            nc.scalar.copy(row[:], bank[:].rearrange("m j p -> m p j"))
+            a_rows.append(row)
+
+        codes_x = [keep.tile([P, S], U32, name=f"codes_x{z}", align_bytes=64) for z in range(PASSES)]
+        nc.vector.tensor_copy(codes_x[0][:], word_win[0][:].bitcast(U32).indirect(offs_t[:]))
+        scales_x = keep.tile([P, S], U8, name="scales_x", align_bytes=64)
+        nc.vector.tensor_copy(scales_x[:], scale_win[:].indirect(offs_t[:]))
+
+        def cast_weights(b):
+            grouped = keep.tile([P, PASSES, P, PACK], BF16, name=f"grouped{b}", align_bytes=64)
+            for z in range(PASSES):
+                nc.scalar.copy(grouped[:, z], w_raw[b, z][:].rearrange("p j c -> p c j"))
+            return grouped
+
+        def quantize_weights(b, grouped):
+            codes = keep.tile([P, PASSES * P], U32, name=f"codes_w{b}", align_bytes=64)
+            scales = keep.tile([P, PASSES * P], U8, name=f"scales_w{b}", align_bytes=64)
+            nc.vector.quantize_mx(
+                out=codes[:].bitcast(FP8X4), scales=scales[:], in_=grouped[:].rearrange("p z c j -> p (z c j)")
+            )
+            return codes, scales
+
+        def product(b, codes, scales, stretches):
+            y = keep.tile([P, S], F32, name=f"y{b}")
+            banks = [
+                psum.tile([P, hi - lo], F32, name=f"acc{b}_{lo}", tag=f"acc{b}_{lo}") for lo, hi in stretches
+            ]
+            for z in range(PASSES):
+                for acc, (lo, hi) in zip(banks, stretches):
+                    nc.tensor.matmul_mx(
+                        out=acc[:],
+                        lhsT=codes[:, z * P : (z + 1) * P].bitcast(FP8X4),
+                        lhsT_scale=scales[:, z * P : (z + 1) * P],
+                        rhs=codes_x[z][:, lo:hi].bitcast(FP8X4),
+                        rhs_scale=scales_x[4 * z : P, lo:hi],
+                        start=(z == 0),
+                        stop=(z == PASSES - 1),
+                    )
+            for acc, (lo, hi) in zip(banks, stretches):
+                nc.scalar.copy(y[:, lo:hi], acc[:])
+            return y
+
+        cut = S - LAST
+        stretches = [(0, BANK), (BANK, cut), (cut, S)]
+        w0 = quantize_weights(0, cast_weights(0))
+        for lo, hi in stretches:
+            nc.vector.tensor_copy(
+                codes_x[1][:, lo:hi], word_win[1][:].bitcast(U32).indirect(offs_t[:, lo // 16 : hi // 16])
+            )
+        w1q = quantize_weights(1, cast_weights(1))
+        y0 = product(0, *w0, stretches)
+        y1 = product(1, *w1q, [(0, BANK), (BANK, S)])
+
+        def weighted(b, y, d):
+            h = keep.tile([P, V], F32, name=f"h{b}{d}")
+            nc.vector.tensor_tensor(
+                h[:], y[:].indirect(pos_t[d][:]), a_rows[d][:].rearrange("m p j -> m (p j)"), ALU.mult
+            )
+            return h
+
+        turned = psum.tile([P, V // P, P], F32, name="turned", tag="t0")
+        for d in range(D):
+            h = weighted(0, y0, d)
+            for i in range(V // P):
+                nc.tensor.matmul(
+                    turned[:, i, :], h[:, i * P : (i + 1) * P], ident[:], is_transpose=True,
+                    start=(d == 0 and i == 0), stop=(d == D - 1 and i == V // P - 1),
+                )
+        turned_sb = keep.tile([P, V // P, P], F32, name="turned_sb")
+        nc.scalar.copy(turned_sb[:], turned[:])
+        back = psum.tile([P, V // P, P], F32, name="back", tag="t1")
+        for i in range(V // P):
+            nc.tensor.transpose(back[:, i, :], turned_sb[:, i, :], ident[:])
+        out0 = keep.tile([P, V], F32, name="out0")
+        nc.scalar.copy(out0[:], back[:].rearrange("m i v -> m (i v)"))
+        nc.scalar.dma_start(out[0:P, :], out0[:])
+
+        h0 = weighted(1, y1, 0)
+        h1 = weighted(1, y1, 1)
+        half = V // 2
+        a_last = a_rows[2][:].rearrange("m p j -> m (p j)")
+        h2 = [keep.tile([P, half], F32, name=f"h12_{i}") for i in range(2)]
+        part = keep.tile([P, V], F32, name="part")
+        for i in range(2):
+            nc.vector.tensor_tensor(
+                h2[i][:],
+                y1[:].indirect(pos_t[2][:, i * half // 16 : (i + 1) * half // 16]),
+                a_last[:, i * half : (i + 1) * half],
+                ALU.mult,
+            )
+            if i == 0:
+                nc.vector.tensor_tensor(part[:], h0[:], h1[:], ALU.add)
+        for i in range(2):
+            out1 = keep.tile([P, half], F32, name=f"out1_{i}")
+            nc.vector.tensor_tensor(out1[:], part[:, i * half : (i + 1) * half], h2[i][:], ALU.add)
+            nc.sync.dma_start(out[P : 2 * P, i * half : (i + 1) * half], out1[:])

@@ -37,35 +37,35 @@ def tile_picked_gatv_none_p_kernel(
         offs_t = lists.tile([P, S // 16], U16, name="offs_t")
         pos_t = [lists.tile([P, V // 16], U16, name=f"pos_t{d}") for d in range(D)]
 
-        scale_win = keep.tile([P, T], U8, name="scale_win", align_bytes=64)
+        scale_win = keep.tile([P, T], U8, name="scale_win", tag="scale_win", align_bytes=64)
         nc.vector.memset(scale_win[:].bitcast(I32), 0)
 
         nc.sync.dma_start(offs_t[:], offs)
         s_t = keep.tile([P, D, 8], F32, name="s_t")
         nc.sync.dma_start(s_t[:, :, 0:4], score[:, 0, :].rearrange("d (p j) -> p d j", j=4))
-        word_win = [keep.tile([P, T], I32, name=f"word_win{z}", align_bytes=64) for z in range(PASSES)]
+        word_win = [keep.tile([P, T], I32, name=f"word_win{z}", tag=f"word_win{z}", align_bytes=64) for z in range(PASSES)]
         w_raw = {}
 
         def load_words(z):
             nc.sync.dma_start(word_win[z][:], x_words[z].rearrange("p c r -> p (c r)").bitcast(I32))
 
-        def load_weights(b):
-            for z in range(PASSES):
-                w_raw[b, z] = keep.tile([P, PACK, P], F32, name=f"w_raw{b}{z}")
-                nc.sync.dma_start(
-                    w_raw[b, z][:],
-                    w1[z * P * PACK : (z + 1) * P * PACK, b * P : (b + 1) * P].rearrange("(p j) c -> p j c", j=PACK),
-                )
+        def load_weights(b, z):
+            w_raw[b, z] = keep.tile([P, PACK, P], F32, name=f"w_raw{b}{z}", tag=f"w_raw{b}{z}", align_bytes=64)
+            nc.sync.dma_start(
+                w_raw[b, z][:],
+                w1[z * P * PACK : (z + 1) * P * PACK, b * P : (b + 1) * P].rearrange("(p j) c -> p j c", j=PACK),
+            )
 
-        load_words(0)
         for q in range(4):
             nc.sync.dma_start(
                 scale_win[32 * q : 32 * q + 8, :].bitcast(I32),
                 x_scales[:, 4 * q : 4 * q + 4, :].bitcast(I32),
             )
-        load_weights(0)
-        load_words(1)
-        load_weights(1)
+        for z in range(PASSES):
+            load_words(z)
+            load_weights(0, z)
+        for z in range(PASSES):
+            load_weights(1, z)
         for d, pos in enumerate((pos1, pos2, pos3)):
             nc.sync.dma_start(pos_t[d][:], pos)
 
@@ -79,74 +79,91 @@ def tile_picked_gatv_none_p_kernel(
 
         s_max = keep.tile([P, 4], F32, name="s_max")
         nc.vector.tensor_reduce(s_max[:], s_t[:, :, 0:4].rearrange("p d j -> p j d"), mybir.AxisListType.X, ALU.max)
-        shifted = keep.tile([P, D, 4], F32, name="shifted")
-        nc.vector.tensor_tensor(shifted[:], s_t[:, :, 0:4], s_max[:].unsqueeze(1).to_broadcast([P, D, 4]), ALU.subtract)
+        neg_max = keep.tile([P, 4], F32, name="neg_max")
+        nc.vector.tensor_scalar(neg_max[:], s_max[:], -1.0, None, ALU.mult)
         e_t = keep.tile([P, D, 4], F32, name="e_t")
-        nc.scalar.activation(e_t[:], shifted[:], ACT.Exp)
         total = keep.tile([P, 4], F32, name="total")
-        nc.vector.tensor_reduce(total[:], e_t[:].rearrange("p d j -> p j d"), mybir.AxisListType.X, ALU.add)
-        inv = keep.tile([P, 4], F32, name="inv")
+        for j in range(4):
+            nc.scalar.activation(
+                e_t[:, :, j], s_t[:, :, j], ACT.Exp, bias=neg_max[:, j : j + 1], accum_out=total[:, j : j + 1]
+            )
+        scales_x = keep.tile([P, S], U8, name="scales_x", align_bytes=64)
+        nc.vector.tensor_copy(scales_x[:], scale_win[:].indirect(offs_t[:]))
+        inv = keep.tile([P, 4], F32, name="inv", tag="scale_win", align_bytes=64)
         nc.vector.reciprocal(inv[:], total[:])
         a_t = keep.tile([P, D, 4], F32, name="a_t")
-        nc.vector.tensor_tensor(a_t[:], e_t[:], inv[:].unsqueeze(1).to_broadcast([P, D, 4]), ALU.mult)
+        for j in range(4):
+            nc.scalar.activation(a_t[:, :, j], e_t[:, :, j], ACT.Copy, scale=inv[:, j : j + 1])
         a_rows = []
-        for d in range(D):
+
+        def spread(d, tag):
             bank = psum.tile([P, 4, P], F32, name=f"spread{d}", tag=f"t{d}")
             for j in range(4):
                 nc.tensor.transpose(bank[:, j, :], a_t[:, d, j : j + 1].to_broadcast([P, P]), ident[:])
-            row = keep.tile([P, P, 4], F32, name=f"a_row{d}")
+            row = keep.tile([P, P, 4], F32, name=f"a_row{d}", tag=tag, align_bytes=64)
             nc.scalar.copy(row[:], bank[:].rearrange("m j p -> m p j"))
             a_rows.append(row)
 
-        codes_x = [keep.tile([P, S], U32, name=f"codes_x{z}", align_bytes=64) for z in range(PASSES)]
-        nc.vector.tensor_copy(codes_x[0][:], word_win[0][:].bitcast(U32).indirect(offs_t[:]))
-        scales_x = keep.tile([P, S], U8, name="scales_x", align_bytes=64)
-        nc.vector.tensor_copy(scales_x[:], scale_win[:].indirect(offs_t[:]))
+        cut = S - LAST
+        stretches = [(0, BANK), (BANK, cut), (cut, S)]
+        codes_x0 = keep.tile([P, S], U32, name="codes_x0", align_bytes=64)
+        nc.vector.tensor_copy(codes_x0[:], word_win[0][:].bitcast(U32).indirect(offs_t[:]))
+        codes_x = [[codes_x0[:, lo:hi] for lo, hi in stretches], []]
 
-        def cast_weights(b):
-            grouped = keep.tile([P, PASSES, P, PACK], BF16, name=f"grouped{b}", align_bytes=64)
-            for z in range(PASSES):
-                nc.scalar.copy(grouped[:, z], w_raw[b, z][:].rearrange("p j c -> p c j"))
-            return grouped
+        def gather_second_pass(lo, hi, tag):
+            piece = keep.tile([P, hi - lo], U32, name=f"codes_x1_{lo}", tag=tag, align_bytes=64)
+            nc.vector.tensor_copy(piece[:], word_win[1][:].bitcast(U32).indirect(offs_t[:, lo // 16 : hi // 16]))
+            codes_x[1].append(piece[:])
 
-        def quantize_weights(b, grouped):
-            codes = keep.tile([P, PASSES * P], U32, name=f"codes_w{b}", align_bytes=64)
-            scales = keep.tile([P, PASSES * P], U8, name=f"scales_w{b}", align_bytes=64)
+        def quantize_weights(b, passes, casts, tag):
+            n = len(passes)
+            grouped = keep.tile([P, n, P, PACK], BF16, name=f"grouped{b}{passes[0]}", tag=tag, align_bytes=64)
+            for i, z in enumerate(passes):
+                casts[i](grouped[:, i], w_raw[b, z][:].rearrange("p j c -> p c j"))
+            codes = keep.tile([P, n * P], U32, name=f"codes_w{b}{passes[0]}", align_bytes=64)
+            scales = keep.tile([P, n * P], U8, name=f"scales_w{b}{passes[0]}", align_bytes=64)
             nc.vector.quantize_mx(
                 out=codes[:].bitcast(FP8X4), scales=scales[:], in_=grouped[:].rearrange("p z c j -> p (z c j)")
             )
-            return codes, scales
+            return [(codes[:, i * P : (i + 1) * P], scales[:, i * P : (i + 1) * P]) for i in range(n)]
 
-        def product(b, codes, scales, stretches):
-            y = keep.tile([P, S], F32, name=f"y{b}")
-            banks = [
-                psum.tile([P, hi - lo], F32, name=f"acc{b}_{lo}", tag=f"acc{b}_{lo}") for lo, hi in stretches
-            ]
-            for z in range(PASSES):
-                for acc, (lo, hi) in zip(banks, stretches):
-                    nc.tensor.matmul_mx(
-                        out=acc[:],
-                        lhsT=codes[:, z * P : (z + 1) * P].bitcast(FP8X4),
-                        lhsT_scale=scales[:, z * P : (z + 1) * P],
-                        rhs=codes_x[z][:, lo:hi].bitcast(FP8X4),
-                        rhs_scale=scales_x[4 * z : P, lo:hi],
-                        start=(z == 0),
-                        stop=(z == PASSES - 1),
-                    )
-            for acc, (lo, hi) in zip(banks, stretches):
-                nc.scalar.copy(y[:, lo:hi], acc[:])
-            return y
-
-        cut = S - LAST
-        stretches = [(0, BANK), (BANK, cut), (cut, S)]
-        w0 = quantize_weights(0, cast_weights(0))
-        for lo, hi in stretches:
-            nc.vector.tensor_copy(
-                codes_x[1][:, lo:hi], word_win[1][:].bitcast(U32).indirect(offs_t[:, lo // 16 : hi // 16])
+        def one_pass(acc, weights, z, i):
+            lo, hi = stretches[i]
+            nc.tensor.matmul_mx(
+                out=acc,
+                lhsT=weights[z][0].bitcast(FP8X4),
+                lhsT_scale=weights[z][1],
+                rhs=codes_x[z][i].bitcast(FP8X4),
+                rhs_scale=scales_x[4 * z : P, lo:hi],
+                start=(z == 0),
+                stop=(z == PASSES - 1),
             )
-        w1q = quantize_weights(1, cast_weights(1))
-        y0 = product(0, *w0, stretches)
-        y1 = product(1, *w1q, [(0, BANK), (BANK, S)])
+
+        w0 = quantize_weights(0, [0], [nc.scalar.copy], "grouped00")
+        spread(0, "w_raw00")
+        spread(1, "grouped00")
+        gather_second_pass(*stretches[0], "piece0")
+        gather_second_pass(*stretches[1], "piece1")
+        w0 = w0 + quantize_weights(0, [1], [nc.scalar.copy], "grouped01")
+        spread(2, "w_raw01")
+        gather_second_pass(*stretches[2], "grouped01")
+        w1q = quantize_weights(1, [0, 1], [nc.vector.tensor_copy, nc.vector.tensor_copy], "word_win1")
+
+        y0 = keep.tile([P, S], F32, name="y0")
+        banks = [psum.tile([P, hi - lo], F32, name=f"acc0_{lo}", tag=f"acc0_{lo}") for lo, hi in stretches]
+        for z in range(PASSES):
+            for i in range(3):
+                one_pass(banks[i][:], w0, z, i)
+        for acc, (lo, hi) in zip(banks, stretches):
+            nc.scalar.copy(y0[:, lo:hi], acc[:])
+
+        y1 = keep.tile([P, S], F32, name="y1")
+        banks = [psum.tile([P, BANK], F32, name=f"acc1_{u}", tag=f"acc1_{u}") for u in range(2)]
+        for i, (lo, hi) in enumerate(stretches):
+            for z in range(PASSES):
+                one_pass(banks[lo // BANK][:, lo % BANK : lo % BANK + hi - lo], w1q, z, i)
+        for u in range(2):
+            nc.scalar.copy(y1[:, u * BANK : (u + 1) * BANK], banks[u][:])
 
         def weighted(b, y, d):
             h = keep.tile([P, V], F32, name=f"h{b}{d}")

@@ -38,36 +38,39 @@ def tile_picked_gatv_none_p_kernel(
         pos_t = [lists.tile([P, V // 16], U16, name=f"pos_t{d}") for d in range(D)]
 
         scale_win = keep.tile([P, T], U8, name="scale_win", tag="scale_win", align_bytes=64)
-        nc.vector.memset(scale_win[:].bitcast(I32), 0)
+        nc.vector.memset(scale_win[32:64, :].bitcast(I32), 0)
+        nc.vector.memset(scale_win[64:P, :].bitcast(I32), 0)
+        planes = keep.tile([P, S], U8, name="planes", align_bytes=64)
+        nc.gpsimd.memset(planes[:].bitcast(I32), 0)
 
-        nc.sync.dma_start(offs_t[:], offs)
         s_t = keep.tile([P, D, 8], F32, name="s_t")
         nc.sync.dma_start(s_t[:, :, 0:4], score[:, 0, :].rearrange("d (p j) -> p d j", j=4))
+        nc.sync.dma_start(offs_t[:], offs)
         word_win = [keep.tile([P, T], I32, name=f"word_win{z}", tag=f"word_win{z}", align_bytes=64) for z in range(PASSES)]
         w_raw = {}
 
         def load_words(z):
             nc.sync.dma_start(word_win[z][:], x_words[z].rearrange("p c r -> p (c r)").bitcast(I32))
 
-        def load_weights(b, z):
-            w_raw[b, z] = keep.tile([P, PACK, P], F32, name=f"w_raw{b}{z}", tag=f"w_raw{b}{z}", align_bytes=64)
+        def load_weights(b, z, tag):
+            w_raw[b, z] = keep.tile([P, PACK, P], F32, name=f"w_raw{b}{z}", tag=tag, align_bytes=64)
             nc.sync.dma_start(
                 w_raw[b, z][:],
                 w1[z * P * PACK : (z + 1) * P * PACK, b * P : (b + 1) * P].rearrange("(p j) c -> p j c", j=PACK),
             )
 
-        for q in range(4):
-            nc.sync.dma_start(
-                scale_win[32 * q : 32 * q + 8, :].bitcast(I32),
-                x_scales[:, 4 * q : 4 * q + 4, :].bitcast(I32),
-            )
-        for z in range(PASSES):
-            load_words(z)
-            load_weights(0, z)
-        for z in range(PASSES):
-            load_weights(1, z)
+        for h in range(2):
+            for z in range(PASSES):
+                nc.sync.dma_start(
+                    scale_win[16 * h + 8 * z : 16 * h + 8 * z + 8, :].bitcast(I32),
+                    x_scales[z, 8 * h : 8 * h + 8, :].bitcast(I32),
+                )
+        load_words(0)
         for d, pos in enumerate((pos1, pos2, pos3)):
             nc.sync.dma_start(pos_t[d][:], pos)
+        load_weights(0, 0, "w_raw00")
+        load_words(1)
+        load_weights(0, 1, "w_raw01")
 
         ident = keep.tile([P, P], F32, name="ident")
         make_identity(nc, ident[:])
@@ -89,11 +92,14 @@ def tile_picked_gatv_none_p_kernel(
             )
         scales_x = keep.tile([P, S], U8, name="scales_x", align_bytes=64)
         nc.vector.tensor_copy(scales_x[:], scale_win[:].indirect(offs_t[:]))
-        inv = keep.tile([P, 4], F32, name="inv", tag="scale_win", align_bytes=64)
+        for q in range(4):
+            first = 16 * (q // 2) + 4 * (q % 2)
+            nc.sync.dma_start(
+                planes[32 * q : 32 * q + 16, :].bitcast(I32), scales_x[first : first + 16, :].bitcast(I32)
+            )
+        load_weights(1, 0, "scale_win")
+        inv = keep.tile([P, 4], F32, name="inv")
         nc.vector.reciprocal(inv[:], total[:])
-        a_t = keep.tile([P, D, 4], F32, name="a_t")
-        for j in range(4):
-            nc.scalar.activation(a_t[:, :, j], e_t[:, :, j], ACT.Copy, scale=inv[:, j : j + 1])
         a_rows = []
 
         def spread(d, tag):
@@ -108,6 +114,7 @@ def tile_picked_gatv_none_p_kernel(
         stretches = [(0, BANK), (BANK, cut), (cut, S)]
         codes_x0 = keep.tile([P, S], U32, name="codes_x0", align_bytes=64)
         nc.vector.tensor_copy(codes_x0[:], word_win[0][:].bitcast(U32).indirect(offs_t[:]))
+        load_weights(1, 1, "word_win0")
         codes_x = [[codes_x0[:, lo:hi] for lo, hi in stretches], []]
 
         def gather_second_pass(lo, hi, tag):
@@ -134,18 +141,20 @@ def tile_picked_gatv_none_p_kernel(
                 lhsT=weights[z][0].bitcast(FP8X4),
                 lhsT_scale=weights[z][1],
                 rhs=codes_x[z][i].bitcast(FP8X4),
-                rhs_scale=scales_x[4 * z : P, lo:hi],
+                rhs_scale=planes[8 * z : P, lo:hi],
                 start=(z == 0),
                 stop=(z == PASSES - 1),
             )
 
         w0 = quantize_weights(0, [0], [nc.scalar.copy], "grouped00")
-        spread(0, "w_raw00")
-        spread(1, "grouped00")
+        a_t = keep.tile([P, D, 4], F32, name="a_t", tag="w_raw00", align_bytes=64)
+        for j in range(4):
+            nc.scalar.activation(a_t[:, :, j], e_t[:, :, j], ACT.Copy, scale=inv[:, j : j + 1])
+        spread(0, "a_row0")
         gather_second_pass(*stretches[0], "piece0")
         gather_second_pass(*stretches[1], "piece1")
         w0 = w0 + quantize_weights(0, [1], [nc.scalar.copy], "grouped01")
-        spread(2, "w_raw01")
+        spread(1, "w_raw01")
         gather_second_pass(*stretches[2], "grouped01")
         w1q = quantize_weights(1, [0, 1], [nc.vector.tensor_copy, nc.vector.tensor_copy], "word_win1")
 
@@ -156,6 +165,7 @@ def tile_picked_gatv_none_p_kernel(
                 one_pass(banks[i][:], w0, z, i)
         for acc, (lo, hi) in zip(banks, stretches):
             nc.scalar.copy(y0[:, lo:hi], acc[:])
+        spread(2, "word_win1")
 
         y1 = keep.tile([P, S], F32, name="y1")
         banks = [psum.tile([P, BANK], F32, name=f"acc1_{u}", tag=f"acc1_{u}") for u in range(2)]

@@ -20,9 +20,15 @@ ACT = mybir.ActivationFunctionType
 P = 128
 PACK = 4
 PASSES = K // (P * PACK)
-BLOCKS = N // P
 BANK = 512
 LAST = 256
+CHUNKS = V // P
+AT_WORDS = 0
+AT_SCALE_WIN = AT_WORDS + 2 * 4 * T
+AT_SCALES_X = AT_SCALE_WIN + T
+AT_CODES_X0 = AT_SCALES_X + S
+AT_GROUPED0 = AT_CODES_X0 + 4 * S
+AT_GROUPED1 = AT_GROUPED0 + 2 * PACK * N
 
 
 def tile_picked_gatv_none_p_kernel(
@@ -32,189 +38,180 @@ def tile_picked_gatv_none_p_kernel(
     with ExitStack() as ctx:
         lists = ctx.enter_context(tc.tile_pool(name="lists", bufs=1))
         keep = ctx.enter_context(tc.tile_pool(name="keep", bufs=1))
+        shared = ctx.enter_context(tc.tile_pool(name="shared", bufs=1))
         psum = ctx.enter_context(tc.psum_pool(name="psum", bufs=1))
+
+        def held(name, shape, dtype, at):
+            return shared.tile(shape, dtype, name=name, offset=at, align_bytes=64)
 
         offs_t = lists.tile([P, S // 16], U16, name="offs_t")
         pos_t = [lists.tile([P, V // 16], U16, name=f"pos_t{d}") for d in range(D)]
 
-        scale_win = keep.tile([P, T], U8, name="scale_win", tag="scale_win", align_bytes=64)
-        nc.vector.memset(scale_win[32:64, :].bitcast(I32), 0)
-        nc.vector.memset(scale_win[64:P, :].bitcast(I32), 0)
-        planes = keep.tile([P, S], U8, name="planes", align_bytes=64)
-        nc.gpsimd.memset(planes[:].bitcast(I32), 0)
+        scale_win = held("scale_win", [P, T], U8, AT_CODES_X0)
+        nc.gpsimd.memset(scale_win[:].bitcast(I32), 0)
+        ident = keep.tile([P, P], F32, name="ident")
+        make_identity(nc, ident[:])
 
         s_t = keep.tile([P, D, 8], F32, name="s_t")
-        nc.sync.dma_start(s_t[:, :, 0:4], score[:, 0, :].rearrange("d (p j) -> p d j", j=4))
+        scores = s_t[:, :, 0:PACK]
+        nc.sync.dma_start(scores, score[:, 0, :].rearrange("d (p j) -> p d j", j=PACK))
         nc.sync.dma_start(offs_t[:], offs)
-        word_win = [keep.tile([P, T], I32, name=f"word_win{z}", tag=f"word_win{z}", align_bytes=64) for z in range(PASSES)]
-        w_raw = {}
+        for q in range(4):
+            nc.sync.dma_start(
+                scale_win[32 * q : 32 * q + 8, :].bitcast(I32), x_scales[:, 4 * q : 4 * q + 4, :].bitcast(I32)
+            )
+        word_win = [held(f"word_win{z}", [P, T], I32, AT_WORDS + 4 * T * z) for z in range(PASSES)]
+        w_raw = []
 
         def load_words(z):
             nc.sync.dma_start(word_win[z][:], x_words[z].rearrange("p c r -> p (c r)").bitcast(I32))
 
-        def load_weights(b, z, tag):
-            w_raw[b, z] = keep.tile([P, PACK, P], F32, name=f"w_raw{b}{z}", tag=tag, align_bytes=64)
+        def load_weights(z):
+            w_raw.append(keep.tile([P, PACK * N], F32, name=f"w_raw{z}", align_bytes=64))
             nc.sync.dma_start(
-                w_raw[b, z][:],
-                w1[z * P * PACK : (z + 1) * P * PACK, b * P : (b + 1) * P].rearrange("(p j) c -> p j c", j=PACK),
+                w_raw[z][:], w1[z * P * PACK : (z + 1) * P * PACK, :].rearrange("(p j) c -> p (j c)", j=PACK)
             )
 
-        for h in range(2):
-            for z in range(PASSES):
-                nc.sync.dma_start(
-                    scale_win[16 * h + 8 * z : 16 * h + 8 * z + 8, :].bitcast(I32),
-                    x_scales[z, 8 * h : 8 * h + 8, :].bitcast(I32),
-                )
+        nc.sync.dma_start(pos_t[0][:], pos1)
         load_words(0)
-        for d, pos in enumerate((pos1, pos2, pos3)):
-            nc.sync.dma_start(pos_t[d][:], pos)
-        load_weights(0, 0, "w_raw00")
+        load_weights(0)
+        load_weights(1)
         load_words(1)
-        load_weights(0, 1, "w_raw01")
+        nc.sync.dma_start(pos_t[1][:], pos2)
+        nc.sync.dma_start(pos_t[2][:], pos3)
 
-        ident = keep.tile([P, P], F32, name="ident")
-        make_identity(nc, ident[:])
-
-        warm = keep.tile([P, 1], F32, name="warm")
-        nc.gpsimd.memset(warm[:], 0.0)
-        warm_out = keep.tile([P, 1], F32, name="warm_out")
-        nc.scalar.activation(warm_out[:], warm[:], ACT.Exp)
-
-        s_max = keep.tile([P, 4], F32, name="s_max")
-        nc.vector.tensor_reduce(s_max[:], s_t[:, :, 0:4].rearrange("p d j -> p j d"), mybir.AxisListType.X, ALU.max)
-        neg_max = keep.tile([P, 4], F32, name="neg_max")
-        nc.vector.tensor_scalar(neg_max[:], s_max[:], -1.0, None, ALU.mult)
-        e_t = keep.tile([P, D, 4], F32, name="e_t")
-        total = keep.tile([P, 4], F32, name="total")
-        for j in range(4):
-            nc.scalar.activation(
-                e_t[:, :, j], s_t[:, :, j], ACT.Exp, bias=neg_max[:, j : j + 1], accum_out=total[:, j : j + 1]
-            )
-        scales_x = keep.tile([P, S], U8, name="scales_x", align_bytes=64)
-        nc.vector.tensor_copy(scales_x[:], scale_win[:].indirect(offs_t[:]))
-        for q in range(4):
-            first = 16 * (q // 2) + 4 * (q % 2)
-            nc.sync.dma_start(
-                planes[32 * q : 32 * q + 16, :].bitcast(I32), scales_x[first : first + 16, :].bitcast(I32)
-            )
-        load_weights(1, 0, "scale_win")
-        inv = keep.tile([P, 4], F32, name="inv")
+        s_max = keep.tile([P, CHUNKS], F32, name="s_max")
+        nc.vector.tensor_reduce(s_max[:], scores.rearrange("p d i -> p i d"), mybir.AxisListType.X, ALU.max)
+        shifted = keep.tile([P, D, CHUNKS], F32, name="shifted")
+        nc.vector.tensor_tensor(
+            shifted[:], scores, s_max[:].unsqueeze(1).to_broadcast([P, D, CHUNKS]), ALU.subtract
+        )
+        e_t = keep.tile([P, D, CHUNKS], F32, name="e_t")
+        total = held("total", [P, CHUNKS], F32, AT_SCALES_X)
+        for i in range(CHUNKS):
+            nc.scalar.activation(e_t[:, :, i], shifted[:, :, i], ACT.Exp, accum_out=total[:, i : i + 1])
+        inv = keep.tile([P, CHUNKS], F32, name="inv")
         nc.vector.reciprocal(inv[:], total[:])
+        scales_x = held("scales_x", [P, S], U8, AT_SCALES_X)
+        nc.vector.tensor_copy(scales_x[:], scale_win[:].indirect(offs_t[:]))
+        a_t = held("a_t", [P, D, 16 + CHUNKS], F32, AT_GROUPED1 - 64)[:, :, 0:CHUNKS]
+        for i in range(CHUNKS):
+            nc.scalar.activation(a_t[:, :, i], e_t[:, :, i], ACT.Copy, scale=inv[:, i : i + 1])
         a_rows = []
-
-        def spread(d, tag):
-            bank = psum.tile([P, 4, P], F32, name=f"spread{d}", tag=f"t{d}")
-            for j in range(4):
-                nc.tensor.transpose(bank[:, j, :], a_t[:, d, j : j + 1].to_broadcast([P, P]), ident[:])
-            row = keep.tile([P, P, 4], F32, name=f"a_row{d}", tag=tag, align_bytes=64)
+        for d in range(D):
+            bank = psum.tile([P, CHUNKS, P], F32, name=f"spread{d}", tag=f"t{d}")
+            for i in range(CHUNKS):
+                nc.tensor.transpose(bank[:, i, :], a_t[:, d, i : i + 1].to_broadcast([P, P]), ident[:])
+            row = keep.tile([P, P, PACK], F32, name=f"a_row{d}")
             nc.scalar.copy(row[:], bank[:].rearrange("m j p -> m p j"))
-            a_rows.append(row)
+            a_rows.append(row[:].rearrange("m p j -> m (p j)"))
+        a_col = keep.tile([P, 2, CHUNKS], F32, name="a_col")
+        for d in range(2):
+            bank = psum.tile([P, CHUNKS, P], F32, name=f"column{d}", tag=f"t{d}")
+            for i in range(CHUNKS):
+                nc.tensor.transpose(bank[:, i, :], a_rows[d][:, i * P : (i + 1) * P], ident[:])
+            nc.scalar.copy(a_col[:, d, :], bank[:, :, 0])
+
+        def gather_words(z, lo, hi, piece):
+            nc.vector.tensor_copy(piece, word_win[z][:].bitcast(U32).indirect(offs_t[:, lo // 16 : hi // 16]))
+            return piece
+
+        def quantize_weights(z, grouped_at, codes_at):
+            grouped = held(f"grouped{z}", [P, N, PACK], BF16, grouped_at)
+            nc.scalar.copy(grouped[:], w_raw[z][:].rearrange("p (j c) -> p c j", j=PACK))
+            codes = held(f"codes_w{z}", [P, N], U32, codes_at)
+            scales = keep.tile([P, N], U8, name=f"scales_w{z}", align_bytes=64)
+            nc.vector.quantize_mx(
+                out=codes[:].bitcast(FP8X4), scales=scales[:], in_=grouped[:].rearrange("p c j -> p (c j)")
+            )
+            return [(codes[:, b * P : (b + 1) * P], scales[:, b * P : (b + 1) * P]) for b in range(2)]
+
+        def one_pass(acc, weights, codes, z, lo, hi, start, stop):
+            nc.tensor.matmul_mx(
+                out=acc,
+                lhsT=weights[0].bitcast(FP8X4),
+                lhsT_scale=weights[1],
+                rhs=codes.bitcast(FP8X4),
+                rhs_scale=scales_x[4 * z : P, lo:hi],
+                start=start,
+                stop=stop,
+            )
 
         cut = S - LAST
         stretches = [(0, BANK), (BANK, cut), (cut, S)]
-        codes_x0 = keep.tile([P, S], U32, name="codes_x0", align_bytes=64)
-        nc.vector.tensor_copy(codes_x0[:], word_win[0][:].bitcast(U32).indirect(offs_t[:]))
-        load_weights(1, 1, "word_win0")
-        codes_x = [[codes_x0[:, lo:hi] for lo, hi in stretches], []]
+        acc = [
+            [psum.tile([P, hi - lo], F32, name=f"acc{b}_{lo}", tag=f"acc{b}_{lo}") for lo, hi in stretches[0:2]]
+            for b in range(2)
+        ]
+        acc[0].append(psum.tile([P, LAST], F32, name="acc0_last", tag="acc0_last"))
+        acc[1].append(psum.tile([P, LAST], F32, name="acc1_last", tag="t2"))
 
-        def gather_second_pass(lo, hi, tag):
-            piece = keep.tile([P, hi - lo], U32, name=f"codes_x1_{lo}", tag=tag, align_bytes=64)
-            nc.vector.tensor_copy(piece[:], word_win[1][:].bitcast(U32).indirect(offs_t[:, lo // 16 : hi // 16]))
-            codes_x[1].append(piece[:])
+        codes_x0 = gather_words(0, 0, S, held("codes_x0", [P, S], U32, AT_CODES_X0)[:])
+        w0 = quantize_weights(0, AT_GROUPED0, AT_WORDS)
+        w1q = quantize_weights(1, AT_GROUPED1, AT_WORDS + 4 * N)
+        for b in range(2):
+            for bank, (lo, hi) in zip(acc[b], stretches):
+                one_pass(bank[:], w0[b], codes_x0[:, lo:hi], 0, lo, hi, True, False)
 
-        def quantize_weights(b, passes, casts, tag):
-            n = len(passes)
-            grouped = keep.tile([P, n, P, PACK], BF16, name=f"grouped{b}{passes[0]}", tag=tag, align_bytes=64)
-            for i, z in enumerate(passes):
-                casts[i](grouped[:, i], w_raw[b, z][:].rearrange("p j c -> p c j"))
-            codes = keep.tile([P, n * P], U32, name=f"codes_w{b}{passes[0]}", align_bytes=64)
-            scales = keep.tile([P, n * P], U8, name=f"scales_w{b}{passes[0]}", align_bytes=64)
-            nc.vector.quantize_mx(
-                out=codes[:].bitcast(FP8X4), scales=scales[:], in_=grouped[:].rearrange("p z c j -> p (z c j)")
-            )
-            return [(codes[:, i * P : (i + 1) * P], scales[:, i * P : (i + 1) * P]) for i in range(n)]
-
-        def one_pass(acc, weights, z, i):
-            lo, hi = stretches[i]
-            nc.tensor.matmul_mx(
-                out=acc,
-                lhsT=weights[z][0].bitcast(FP8X4),
-                lhsT_scale=weights[z][1],
-                rhs=codes_x[z][i].bitcast(FP8X4),
-                rhs_scale=planes[8 * z : P, lo:hi],
-                start=(z == 0),
-                stop=(z == PASSES - 1),
-            )
-
-        w0 = quantize_weights(0, [0], [nc.scalar.copy], "grouped00")
-        a_t = keep.tile([P, D, 4], F32, name="a_t", tag="w_raw00", align_bytes=64)
-        for j in range(4):
-            nc.scalar.activation(a_t[:, :, j], e_t[:, :, j], ACT.Copy, scale=inv[:, j : j + 1])
-        spread(0, "a_row0")
-        gather_second_pass(*stretches[0], "piece0")
-        gather_second_pass(*stretches[1], "piece1")
-        w0 = w0 + quantize_weights(0, [1], [nc.scalar.copy], "grouped01")
-        spread(1, "w_raw01")
-        gather_second_pass(*stretches[2], "grouped01")
-        w1q = quantize_weights(1, [0, 1], [nc.vector.tensor_copy, nc.vector.tensor_copy], "word_win1")
-
-        y0 = keep.tile([P, S], F32, name="y0")
-        banks = [psum.tile([P, hi - lo], F32, name=f"acc0_{lo}", tag=f"acc0_{lo}") for lo, hi in stretches]
-        for z in range(PASSES):
-            for i in range(3):
-                one_pass(banks[i][:], w0, z, i)
-        for acc, (lo, hi) in zip(banks, stretches):
-            nc.scalar.copy(y0[:, lo:hi], acc[:])
-        spread(2, "word_win1")
-
-        y1 = keep.tile([P, S], F32, name="y1")
-        banks = [psum.tile([P, BANK], F32, name=f"acc1_{u}", tag=f"acc1_{u}") for u in range(2)]
+        codes_x1 = held("codes_x1", [P, S], U32, AT_GROUPED1)
+        y = [keep.tile([P, S], F32, name=f"y{b}") for b in range(2)]
+        copies = [
+            [nc.scalar.copy, nc.scalar.copy], [nc.scalar.copy, nc.vector.tensor_copy],
+            [nc.scalar.copy, nc.vector.tensor_copy],
+        ]
+        for lo, hi in stretches:
+            gather_words(1, lo, hi, codes_x1[:, lo:hi])
         for i, (lo, hi) in enumerate(stretches):
-            for z in range(PASSES):
-                one_pass(banks[lo // BANK][:, lo % BANK : lo % BANK + hi - lo], w1q, z, i)
-        for u in range(2):
-            nc.scalar.copy(y1[:, u * BANK : (u + 1) * BANK], banks[u][:])
+            for b in range(2):
+                one_pass(acc[b][i][:], w1q[b], codes_x1[:, lo:hi], 1, lo, hi, False, True)
+        for i, (lo, hi) in enumerate(stretches):
+            for b in range(2):
+                copies[i][b](y[b][:, lo:hi], acc[b][i][:])
 
-        def weighted(b, y, d):
+        def weighted(b, d):
             h = keep.tile([P, V], F32, name=f"h{b}{d}")
-            nc.vector.tensor_tensor(
-                h[:], y[:].indirect(pos_t[d][:]), a_rows[d][:].rearrange("m p j -> m (p j)"), ALU.mult
-            )
+            nc.vector.tensor_tensor(h[:], y[b][:].indirect(pos_t[d][:]), a_rows[d], ALU.mult)
             return h
 
-        turned = psum.tile([P, V // P, P], F32, name="turned", tag="t0")
-        for d in range(D):
-            h = weighted(0, y0, d)
-            for i in range(V // P):
-                nc.tensor.matmul(
-                    turned[:, i, :], h[:, i * P : (i + 1) * P], ident[:], is_transpose=True,
-                    start=(d == 0 and i == 0), stop=(d == D - 1 and i == V // P - 1),
-                )
-        turned_sb = keep.tile([P, V // P, P], F32, name="turned_sb")
-        nc.scalar.copy(turned_sb[:], turned[:])
-        back = psum.tile([P, V // P, P], F32, name="back", tag="t1")
-        for i in range(V // P):
-            nc.tensor.transpose(back[:, i, :], turned_sb[:, i, :], ident[:])
-        out0 = keep.tile([P, V], F32, name="out0")
-        nc.scalar.copy(out0[:], back[:].rearrange("m i v -> m (i v)"))
-        nc.scalar.dma_start(out[0:P, :], out0[:])
+        def plain(b, d):
+            g = held(f"g{b}{d}", [P, V], F32, AT_WORDS + 4 * T + 4 * V * (d % 2))
+            nc.scalar.activation(g[:], y[b][:].indirect(pos_t[d][:]), ACT.Copy)
+            return g
 
-        h0 = weighted(1, y1, 0)
-        h1 = weighted(1, y1, 1)
+        h02 = weighted(0, 2)
+        turned = []
+        for d in range(2):
+            g = plain(0, d)
+            bank = psum.tile([P, CHUNKS, P], F32, name=f"turned{d}", tag=f"t{d}")
+            for i in range(CHUNKS):
+                nc.tensor.transpose(bank[:, i, :], g[:, i * P : (i + 1) * P], ident[:])
+            turned.append(bank)
+        g12 = plain(1, 2)
         half = V // 2
-        a_last = a_rows[2][:].rearrange("m p j -> m (p j)")
-        h2 = [keep.tile([P, half], F32, name=f"h12_{i}") for i in range(2)]
+        back = [psum.tile([P, 2, P], F32, name=f"back{u}", tag=f"acc{u}_0") for u in range(2)]
+        for u in range(2):
+            for d in range(2):
+                scaled = keep.tile([P, 2, P], F32, name=f"scaled{u}{d}")
+                for i in range(2):
+                    c = 2 * u + i
+                    nc.scalar.activation(scaled[:, i, :], turned[d][:, c, :], ACT.Copy, scale=a_col[:, d, c : c + 1])
+                for i in range(2):
+                    nc.tensor.matmul(
+                        back[u][:, i, :], scaled[:, i, :], ident[:], is_transpose=True,
+                        start=(d == 0 and i == 0), stop=(d == 1 and i == 1),
+                    )
+
+        h10 = weighted(1, 0)
+        h11 = weighted(1, 1)
         part = keep.tile([P, V], F32, name="part")
-        for i in range(2):
-            nc.vector.tensor_tensor(
-                h2[i][:],
-                y1[:].indirect(pos_t[2][:, i * half // 16 : (i + 1) * half // 16]),
-                a_last[:, i * half : (i + 1) * half],
-                ALU.mult,
-            )
-            if i == 0:
-                nc.vector.tensor_tensor(part[:], h0[:], h1[:], ALU.add)
-        for i in range(2):
-            out1 = keep.tile([P, half], F32, name=f"out1_{i}")
-            nc.vector.tensor_tensor(out1[:], part[:, i * half : (i + 1) * half], h2[i][:], ALU.add)
-            nc.sync.dma_start(out[P : 2 * P, i * half : (i + 1) * half], out1[:])
+        nc.vector.tensor_tensor(part[:], h10[:], h11[:], ALU.add)
+        h12 = keep.tile([P, V], F32, name="h12")
+        nc.vector.tensor_tensor(h12[:], g12[:], a_rows[2], ALU.mult)
+        out1 = keep.tile([P, V], F32, name="out1")
+        nc.vector.tensor_tensor(out1[:], part[:], h12[:], ALU.add)
+        nc.sync.dma_start(out[P : 2 * P, :], out1[:])
+        for u in range(2):
+            cols = slice(u * half, (u + 1) * half)
+            out0 = keep.tile([P, half], F32, name=f"out0_{u}")
+            nc.vector.tensor_tensor(out0[:], back[u][:].rearrange("m i v -> m (i v)"), h02[:, cols], ALU.add)
+            nc.sync.dma_start(out[0:P, cols], out0[:])

@@ -21,14 +21,17 @@ P = 128
 PACK = 4
 PASSES = K // (P * PACK)
 BANK = 512
-LAST = 256
+PIECE = 256
 CHUNKS = V // P
 AT_WORDS = 0
 AT_SCALE_WIN = AT_WORDS + 2 * 4 * T
-AT_SCALES_X = AT_SCALE_WIN + T
-AT_CODES_X0 = AT_SCALES_X + S
-AT_GROUPED0 = AT_CODES_X0 + 4 * S
-AT_GROUPED1 = AT_GROUPED0 + 2 * PACK * N
+AT_SCALES_X = AT_SCALE_WIN + 64 + 4 * PACK * N
+AT_CODES_W0 = AT_SCALES_X + S
+AT_CODES_W1 = AT_CODES_W0 + 4 * N
+AT_GROUPED0 = AT_CODES_W1 + 4 * N
+AT_GROUPED1 = AT_GROUPED0 + 4 * S
+AT_Y1 = AT_GROUPED1 + 2 * PACK * N
+AT_W0 = AT_Y1 + 4 * S
 
 
 def tile_picked_gatv_none_p_kernel(
@@ -47,8 +50,11 @@ def tile_picked_gatv_none_p_kernel(
         offs_t = lists.tile([P, S // 16], U16, name="offs_t")
         pos_t = [lists.tile([P, V // 16], U16, name=f"pos_t{d}") for d in range(D)]
 
-        scale_win = held("scale_win", [P, T], U8, AT_CODES_X0)
-        nc.gpsimd.memset(scale_win[:].bitcast(I32), 0)
+        scale_win = held("scale_win", [P, T], U8, AT_SCALE_WIN + 1024)
+        nc.vector.memset(scale_win[32:64, :].bitcast(I32), 0)
+        nc.vector.memset(scale_win[64:P, :].bitcast(I32), 0)
+        planes = keep.tile([P, S], U8, name="planes", align_bytes=64)
+        nc.gpsimd.memset(planes[:].bitcast(I32), 0)
         ident = keep.tile([P, P], F32, name="ident")
         make_identity(nc, ident[:])
 
@@ -56,45 +62,63 @@ def tile_picked_gatv_none_p_kernel(
         scores = s_t[:, :, 0:PACK]
         nc.sync.dma_start(scores, score[:, 0, :].rearrange("d (p j) -> p d j", j=PACK))
         nc.sync.dma_start(offs_t[:], offs)
-        for q in range(4):
-            nc.sync.dma_start(
-                scale_win[32 * q : 32 * q + 8, :].bitcast(I32), x_scales[:, 4 * q : 4 * q + 4, :].bitcast(I32)
-            )
+        for h in range(2):
+            for z in range(PASSES):
+                nc.sync.dma_start(
+                    scale_win[16 * h + 8 * z : 16 * h + 8 * z + 8, :].bitcast(I32),
+                    x_scales[z, 8 * h : 8 * h + 8, :].bitcast(I32),
+                )
         word_win = [held(f"word_win{z}", [P, T], I32, AT_WORDS + 4 * T * z) for z in range(PASSES)]
         w_raw = []
 
         def load_words(z):
             nc.sync.dma_start(word_win[z][:], x_words[z].rearrange("p c r -> p (c r)").bitcast(I32))
 
-        def load_weights(z):
-            w_raw.append(keep.tile([P, PACK * N], F32, name=f"w_raw{z}", align_bytes=64))
+        def load_weights(z, at):
+            w_raw.append(held(f"w_raw{z}", [P, PACK * N], F32, at))
             nc.sync.dma_start(
                 w_raw[z][:], w1[z * P * PACK : (z + 1) * P * PACK, :].rearrange("(p j) c -> p (j c)", j=PACK)
             )
 
-        nc.sync.dma_start(pos_t[0][:], pos1)
+        load_weights(0, AT_W0)
         load_words(0)
-        load_weights(0)
-        load_weights(1)
+        for d, pos in enumerate((pos1, pos2, pos3)):
+            nc.sync.dma_start(pos_t[d][:], pos)
         load_words(1)
-        nc.sync.dma_start(pos_t[1][:], pos2)
-        nc.sync.dma_start(pos_t[2][:], pos3)
 
         s_max = keep.tile([P, CHUNKS], F32, name="s_max")
         nc.vector.tensor_reduce(s_max[:], scores.rearrange("p d i -> p i d"), mybir.AxisListType.X, ALU.max)
-        shifted = keep.tile([P, D, CHUNKS], F32, name="shifted")
+        shifted = held("shifted", [P, D, CHUNKS], F32, AT_GROUPED0)
         nc.vector.tensor_tensor(
             shifted[:], scores, s_max[:].unsqueeze(1).to_broadcast([P, D, CHUNKS]), ALU.subtract
         )
         e_t = keep.tile([P, D, CHUNKS], F32, name="e_t")
-        total = held("total", [P, CHUNKS], F32, AT_SCALES_X)
+        total = keep.tile([P, CHUNKS], F32, name="total")
         for i in range(CHUNKS):
             nc.scalar.activation(e_t[:, :, i], shifted[:, :, i], ACT.Exp, accum_out=total[:, i : i + 1])
-        inv = keep.tile([P, CHUNKS], F32, name="inv")
-        nc.vector.reciprocal(inv[:], total[:])
+
+        def cast(name, rows, at):
+            grouped = held(name, list(rows.shape), BF16, at)
+            nc.scalar.copy(grouped[:], rows)
+            return grouped
+
+        grouped0 = cast("grouped0", w_raw[0][:].rearrange("p (j c) -> p c j", j=PACK), AT_GROUPED0)
         scales_x = held("scales_x", [P, S], U8, AT_SCALES_X)
         nc.vector.tensor_copy(scales_x[:], scale_win[:].indirect(offs_t[:]))
-        a_t = held("a_t", [P, D, 16 + CHUNKS], F32, AT_GROUPED1 - 64)[:, :, 0:CHUNKS]
+        inv = held("inv", [P, CHUNKS], F32, AT_SCALE_WIN + 2048)
+        nc.vector.reciprocal(inv[:], total[:])
+        for q in range(4):
+            first = 16 * (q // 2) + 4 * (q % 2)
+            nc.sync.dma_start(
+                planes[32 * q : 32 * q + 16, :].bitcast(I32), scales_x[first : first + 16, :].bitcast(I32)
+            )
+        late = []
+        for b in range(2):
+            late.append(held(f"w_late{b}", [P, PACK, P], F32, AT_SCALE_WIN + 2112 * b))
+            nc.sync.dma_start(
+                late[b][:], w1[P * PACK : K, b * P : (b + 1) * P].rearrange("(p j) c -> p j c", j=PACK)
+            )
+        a_t = held("a_t", [P, D, CHUNKS], F32, AT_W0)
         for i in range(CHUNKS):
             nc.scalar.activation(a_t[:, :, i], e_t[:, :, i], ACT.Copy, scale=inv[:, i : i + 1])
         a_rows = []
@@ -105,26 +129,19 @@ def tile_picked_gatv_none_p_kernel(
             row = keep.tile([P, P, PACK], F32, name=f"a_row{d}")
             nc.scalar.copy(row[:], bank[:].rearrange("m j p -> m p j"))
             a_rows.append(row[:].rearrange("m p j -> m (p j)"))
-        a_col = keep.tile([P, 2, CHUNKS], F32, name="a_col")
-        for d in range(2):
-            bank = psum.tile([P, CHUNKS, P], F32, name=f"column{d}", tag=f"t{d}")
-            for i in range(CHUNKS):
-                nc.tensor.transpose(bank[:, i, :], a_rows[d][:, i * P : (i + 1) * P], ident[:])
-            nc.scalar.copy(a_col[:, d, :], bank[:, :, 0])
 
         def gather_words(z, lo, hi, piece):
             nc.vector.tensor_copy(piece, word_win[z][:].bitcast(U32).indirect(offs_t[:, lo // 16 : hi // 16]))
             return piece
 
-        def quantize_weights(z, grouped_at, codes_at):
-            grouped = held(f"grouped{z}", [P, N, PACK], BF16, grouped_at)
-            nc.scalar.copy(grouped[:], w_raw[z][:].rearrange("p (j c) -> p c j", j=PACK))
-            codes = held(f"codes_w{z}", [P, N], U32, codes_at)
-            scales = keep.tile([P, N], U8, name=f"scales_w{z}", align_bytes=64)
+        def quantize(n, grouped, at):
+            width = grouped.shape[1]
+            codes = held(f"codes_w{n}", [P, width], U32, at)
+            scales = keep.tile([P, width], U8, name=f"scales_w{n}", align_bytes=64)
             nc.vector.quantize_mx(
                 out=codes[:].bitcast(FP8X4), scales=scales[:], in_=grouped[:].rearrange("p c j -> p (c j)")
             )
-            return [(codes[:, b * P : (b + 1) * P], scales[:, b * P : (b + 1) * P]) for b in range(2)]
+            return [(codes[:, c : c + P], scales[:, c : c + P]) for c in range(0, width, P)]
 
         def one_pass(acc, weights, codes, z, lo, hi, start, stop):
             nc.tensor.matmul_mx(
@@ -132,41 +149,44 @@ def tile_picked_gatv_none_p_kernel(
                 lhsT=weights[0].bitcast(FP8X4),
                 lhsT_scale=weights[1],
                 rhs=codes.bitcast(FP8X4),
-                rhs_scale=scales_x[4 * z : P, lo:hi],
+                rhs_scale=planes[8 * z : P, lo:hi],
                 start=start,
                 stop=stop,
             )
 
-        cut = S - LAST
+        cut = S - PIECE
         stretches = [(0, BANK), (BANK, cut), (cut, S)]
+        tags = [["acc0_0", "acc0_1", "acc0_2"], ["acc1_0", "acc1_1", "t2"]]
         acc = [
-            [psum.tile([P, hi - lo], F32, name=f"acc{b}_{lo}", tag=f"acc{b}_{lo}") for lo, hi in stretches[0:2]]
+            [psum.tile([P, hi - lo], F32, name=f"acc{b}_{lo}", tag=tag) for tag, (lo, hi) in zip(tags[b], stretches)]
             for b in range(2)
         ]
-        acc[0].append(psum.tile([P, LAST], F32, name="acc0_last", tag="acc0_last"))
-        acc[1].append(psum.tile([P, LAST], F32, name="acc1_last", tag="t2"))
 
-        codes_x0 = gather_words(0, 0, S, held("codes_x0", [P, S], U32, AT_CODES_X0)[:])
-        w0 = quantize_weights(0, AT_GROUPED0, AT_WORDS)
-        w1q = quantize_weights(1, AT_GROUPED1, AT_WORDS + 4 * N)
+        w0 = quantize(0, grouped0, AT_CODES_W0)
+        codes_x0 = gather_words(0, 0, S, keep.tile([P, S], U32, name="codes_x0", align_bytes=64)[:])
         for b in range(2):
             for bank, (lo, hi) in zip(acc[b], stretches):
                 one_pass(bank[:], w0[b], codes_x0[:, lo:hi], 0, lo, hi, True, False)
 
-        codes_x1 = held("codes_x1", [P, S], U32, AT_GROUPED1)
+        grouped = [cast(f"grouped1{b}", late[b][:].rearrange("p j c -> p c j"), AT_GROUPED1 + 1024 * b) for b in range(2)]
+        codes_x1 = [gather_words(1, 0, BANK, keep.tile([P, BANK], U32, name="codes_x1_0", align_bytes=64)[:])]
+        w1q = quantize(1, grouped[0], AT_CODES_W1)
+        codes_x1.append(gather_words(1, BANK, cut, held("codes_x1_1", [P, PIECE], U32, AT_SCALE_WIN)[:]))
+        w1q = w1q + quantize(2, grouped[1], AT_CODES_W1 + 512)
+        codes_x1.append(gather_words(1, cut, S, held("codes_x1_2", [P, PIECE], U32, AT_SCALE_WIN + 2112)[:]))
         y = [keep.tile([P, S], F32, name=f"y{b}") for b in range(2)]
-        copies = [
-            [nc.scalar.copy, nc.scalar.copy], [nc.scalar.copy, nc.vector.tensor_copy],
-            [nc.scalar.copy, nc.vector.tensor_copy],
-        ]
-        for lo, hi in stretches:
-            gather_words(1, lo, hi, codes_x1[:, lo:hi])
-        for i, (lo, hi) in enumerate(stretches):
-            for b in range(2):
-                one_pass(acc[b][i][:], w1q[b], codes_x1[:, lo:hi], 1, lo, hi, False, True)
-        for i, (lo, hi) in enumerate(stretches):
-            for b in range(2):
-                copies[i][b](y[b][:, lo:hi], acc[b][i][:])
+        for b, i in ((0, 0), (0, 1), (0, 2), (1, 0), (1, 1), (1, 2)):
+            one_pass(acc[b][i][:], w1q[b], codes_x1[i], 1, *stretches[i], False, True)
+        for b, i in ((0, 0), (0, 1), (0, 2), (1, 0), (1, 1), (1, 2)):
+            lo, hi = stretches[i]
+            copy = nc.vector.tensor_copy if (b, i) == (0, 2) else nc.scalar.copy
+            copy(y[b][:, lo:hi], acc[b][i][:])
+        a_col = keep.tile([P, 2, CHUNKS], F32, name="a_col")
+        for d in range(2):
+            bank = psum.tile([P, CHUNKS, P], F32, name=f"column{d}", tag=f"acc{d}_0")
+            for i in range(CHUNKS):
+                nc.tensor.transpose(bank[:, i, :], a_rows[d][:, i * P : (i + 1) * P], ident[:])
+            nc.scalar.copy(a_col[:, d, :], bank[:, :, 0])
 
         def weighted(b, d):
             h = keep.tile([P, V], F32, name=f"h{b}{d}")
@@ -174,21 +194,23 @@ def tile_picked_gatv_none_p_kernel(
             return h
 
         def plain(b, d):
-            g = held(f"g{b}{d}", [P, V], F32, AT_WORDS + 4 * T + 4 * V * (d % 2))
+            g = held(f"g{b}{d}", [P, V], F32, AT_Y1 + 4 * V * (d % 2))
             nc.scalar.activation(g[:], y[b][:].indirect(pos_t[d][:]), ACT.Copy)
             return g
 
-        h02 = weighted(0, 2)
+        h00 = weighted(0, 0)
+        h01 = weighted(0, 1)
+        h12 = weighted(1, 2)
         turned = []
         for d in range(2):
-            g = plain(0, d)
+            g = plain(1, d)
             bank = psum.tile([P, CHUNKS, P], F32, name=f"turned{d}", tag=f"t{d}")
             for i in range(CHUNKS):
                 nc.tensor.transpose(bank[:, i, :], g[:, i * P : (i + 1) * P], ident[:])
             turned.append(bank)
-        g12 = plain(1, 2)
+        g02 = plain(0, 2)
         half = V // 2
-        back = [psum.tile([P, 2, P], F32, name=f"back{u}", tag=f"acc{u}_0") for u in range(2)]
+        back = [psum.tile([P, 2, P], F32, name=f"back{u}", tag=f"acc{u}_1") for u in range(2)]
         for u in range(2):
             for d in range(2):
                 scaled = keep.tile([P, 2, P], F32, name=f"scaled{u}{d}")
@@ -201,17 +223,18 @@ def tile_picked_gatv_none_p_kernel(
                         start=(d == 0 and i == 0), stop=(d == 1 and i == 1),
                     )
 
-        h10 = weighted(1, 0)
-        h11 = weighted(1, 1)
-        part = keep.tile([P, V], F32, name="part")
-        nc.vector.tensor_tensor(part[:], h10[:], h11[:], ALU.add)
-        h12 = keep.tile([P, V], F32, name="h12")
-        nc.vector.tensor_tensor(h12[:], g12[:], a_rows[2], ALU.mult)
-        out1 = keep.tile([P, V], F32, name="out1")
-        nc.vector.tensor_tensor(out1[:], part[:], h12[:], ALU.add)
-        nc.sync.dma_start(out[P : 2 * P, :], out1[:])
-        for u in range(2):
+        def finish_block1(u):
             cols = slice(u * half, (u + 1) * half)
-            out0 = keep.tile([P, half], F32, name=f"out0_{u}")
-            nc.vector.tensor_tensor(out0[:], back[u][:].rearrange("m i v -> m (i v)"), h02[:, cols], ALU.add)
-            nc.sync.dma_start(out[0:P, cols], out0[:])
+            out1 = keep.tile([P, half], F32, name=f"out1_{u}")
+            nc.vector.tensor_tensor(out1[:], back[u][:].rearrange("m i v -> m (i v)"), h12[:, cols], ALU.add)
+            nc.sync.dma_start(out[P : 2 * P, cols], out1[:])
+
+        part = keep.tile([P, V], F32, name="part")
+        nc.vector.tensor_tensor(part[:], h00[:], h01[:], ALU.add)
+        h02 = keep.tile([P, V], F32, name="h02")
+        nc.vector.tensor_tensor(h02[:], g02[:], a_rows[2], ALU.mult)
+        out0 = keep.tile([P, V], F32, name="out0")
+        nc.vector.tensor_tensor(out0[:], part[:], h02[:], ALU.add)
+        nc.sync.dma_start(out[0:P, :], out0[:])
+        finish_block1(0)
+        finish_block1(1)

@@ -20,18 +20,20 @@ ACT = mybir.ActivationFunctionType
 P = 128
 PACK = 4
 PASSES = K // (P * PACK)
+BLOCKS = N // P
 BANK = 512
-PIECE = 256
 CHUNKS = V // P
-AT_WORDS = 0
-AT_SCALE_WIN = AT_WORDS + 2 * 4 * T
-AT_SCALES_X = AT_SCALE_WIN + 64 + 4 * PACK * N
-AT_CODES_W0 = AT_SCALES_X + S
-AT_CODES_W1 = AT_CODES_W0 + 4 * N
-AT_GROUPED0 = AT_CODES_W1 + 4 * N
-AT_GROUPED1 = AT_GROUPED0 + 4 * S
-AT_Y1 = AT_GROUPED1 + 2 * PACK * N
-AT_W0 = AT_Y1 + 4 * S
+HALF = V // 2
+PIECE = 256
+GAP = 12
+CLEARED_BY_GPSIMD = 3 * T // 4
+
+QUARTER = 4 * PACK * P
+AT_LATE = 0
+AT_SCALE_WINDOW = AT_LATE + QUARTER // 2
+AT_ROW2 = AT_LATE + 3 * QUARTER // 2
+AT_GROUPED0 = AT_ROW2 + 4 * V
+AT_RAW0 = AT_GROUPED0 + 2 * PACK * N
 
 
 def tile_picked_gatv_none_p_kernel(
@@ -41,200 +43,217 @@ def tile_picked_gatv_none_p_kernel(
     with ExitStack() as ctx:
         lists = ctx.enter_context(tc.tile_pool(name="lists", bufs=1))
         keep = ctx.enter_context(tc.tile_pool(name="keep", bufs=1))
-        shared = ctx.enter_context(tc.tile_pool(name="shared", bufs=1))
+        reused = ctx.enter_context(tc.tile_pool(name="reused", bufs=1))
         psum = ctx.enter_context(tc.psum_pool(name="psum", bufs=1))
 
-        def held(name, shape, dtype, at):
-            return shared.tile(shape, dtype, name=name, offset=at, align_bytes=64)
+        def placed(name, shape, dtype, at):
+            return reused.tile(shape, dtype, name=name, offset=at, align_bytes=64)
 
         offs_t = lists.tile([P, S // 16], U16, name="offs_t")
         pos_t = [lists.tile([P, V // 16], U16, name=f"pos_t{d}") for d in range(D)]
 
-        scale_win = held("scale_win", [P, T], U8, AT_SCALE_WIN + 1024)
-        nc.vector.memset(scale_win[32:64, :].bitcast(I32), 0)
-        nc.vector.memset(scale_win[64:P, :].bitcast(I32), 0)
+        scale_window = placed("scale_window", [P, T], U8, AT_SCALE_WINDOW)
+        nc.gpsimd.memset(scale_window[:, 0:CLEARED_BY_GPSIMD].bitcast(I32), 0)
+        nc.vector.memset(scale_window[:, CLEARED_BY_GPSIMD:T].bitcast(I32), 0)
         planes = keep.tile([P, S], U8, name="planes", align_bytes=64)
         nc.gpsimd.memset(planes[:].bitcast(I32), 0)
         ident = keep.tile([P, P], F32, name="ident")
         make_identity(nc, ident[:])
 
-        s_t = keep.tile([P, D, 8], F32, name="s_t")
-        scores = s_t[:, :, 0:PACK]
+        score_tile = keep.tile([P, D, 2 * PACK], F32, name="score_tile")
+        scores = score_tile[:, :, 0:PACK]
         nc.sync.dma_start(scores, score[:, 0, :].rearrange("d (p j) -> p d j", j=PACK))
         nc.sync.dma_start(offs_t[:], offs)
+        nc.sync.dma_start(pos_t[0][:], pos1)
         for h in range(2):
             for z in range(PASSES):
-                nc.sync.dma_start(
-                    scale_win[16 * h + 8 * z : 16 * h + 8 * z + 8, :].bitcast(I32),
-                    x_scales[z, 8 * h : 8 * h + 8, :].bitcast(I32),
+                first = 32 * h + GAP * z
+                (nc.scalar if (h, z) == (1, PASSES - 1) else nc.sync).dma_start(
+                    scale_window[first : first + 8, :].bitcast(I32), x_scales[z, 8 * h : 8 * h + 8, :].bitcast(I32)
                 )
-        word_win = [held(f"word_win{z}", [P, T], I32, AT_WORDS + 4 * T * z) for z in range(PASSES)]
-        w_raw = []
+        word_window = [keep.tile([P, T], I32, name=f"word_window{z}", align_bytes=64) for z in range(PASSES)]
 
         def load_words(z):
-            nc.sync.dma_start(word_win[z][:], x_words[z].rearrange("p c r -> p (c r)").bitcast(I32))
+            nc.sync.dma_start(word_window[z][:], x_words[z].rearrange("p c r -> p (c r)").bitcast(I32))
 
-        def load_weights(z, at):
-            w_raw.append(held(f"w_raw{z}", [P, PACK * N], F32, at))
-            nc.sync.dma_start(
-                w_raw[z][:], w1[z * P * PACK : (z + 1) * P * PACK, :].rearrange("(p j) c -> p (j c)", j=PACK)
+        load_words(0)
+        raw0 = placed("raw0", [P, PACK * N], F32, AT_RAW0)
+        nc.sync.dma_start(raw0[:], w1[0 : P * PACK, :].rearrange("(p j) c -> p (j c)", j=PACK))
+        nc.sync.dma_start(pos_t[1][:], pos2)
+        load_words(1)
+        nc.sync.dma_start(pos_t[2][:], pos3)
+
+        neg_scores = keep.tile([P, D, PACK], F32, name="neg_scores")
+        nc.scalar.activation(neg_scores[:], scores, ACT.Copy, scale=-1.0)
+        neg_max = keep.tile([P, PACK], F32, name="neg_max")
+        nc.vector.tensor_reduce(
+            neg_max[:], scores.rearrange("p d j -> p j d"), mybir.AxisListType.X, ALU.max, negate=True
+        )
+        exps = placed("exps", [P, D, PACK], F32, AT_GROUPED0)
+        total = keep.tile([P, PACK], F32, name="total")
+        for j in range(PACK):
+            nc.scalar.activation(
+                exps[:, :, j], neg_scores[:, :, j], ACT.Exp, scale=-1.0, bias=neg_max[:, j : j + 1],
+                accum_out=total[:, j : j + 1],
             )
 
-        load_weights(0, AT_W0)
-        load_words(0)
-        for d, pos in enumerate((pos1, pos2, pos3)):
-            nc.sync.dma_start(pos_t[d][:], pos)
-        load_words(1)
-
-        s_max = keep.tile([P, CHUNKS], F32, name="s_max")
-        nc.vector.tensor_reduce(s_max[:], scores.rearrange("p d i -> p i d"), mybir.AxisListType.X, ALU.max)
-        shifted = held("shifted", [P, D, CHUNKS], F32, AT_GROUPED0)
-        nc.vector.tensor_tensor(
-            shifted[:], scores, s_max[:].unsqueeze(1).to_broadcast([P, D, CHUNKS]), ALU.subtract
-        )
-        e_t = keep.tile([P, D, CHUNKS], F32, name="e_t")
-        total = keep.tile([P, CHUNKS], F32, name="total")
-        for i in range(CHUNKS):
-            nc.scalar.activation(e_t[:, :, i], shifted[:, :, i], ACT.Exp, accum_out=total[:, i : i + 1])
-
-        def cast(name, rows, at):
-            grouped = held(name, list(rows.shape), BF16, at)
-            nc.scalar.copy(grouped[:], rows)
-            return grouped
-
-        grouped0 = cast("grouped0", w_raw[0][:].rearrange("p (j c) -> p c j", j=PACK), AT_GROUPED0)
-        scales_x = held("scales_x", [P, S], U8, AT_SCALES_X)
-        nc.vector.tensor_copy(scales_x[:], scale_win[:].indirect(offs_t[:]))
-        inv = held("inv", [P, CHUNKS], F32, AT_SCALE_WIN + 2048)
-        nc.vector.reciprocal(inv[:], total[:])
+        scales_x = keep.tile([P, S], U8, name="scales_x", align_bytes=64)
+        nc.vector.tensor_copy(scales_x[:], scale_window[:].indirect(offs_t[:]))
+        root = keep.tile([P, PACK], F32, name="root")
+        nc.scalar.activation(root[:], total[:], ACT.Abs_reciprocal_sqrt)
+        inverse = keep.tile([P, PACK], F32, name="inverse")
+        nc.scalar.activation(inverse[:], root[:], ACT.Square)
         for q in range(4):
-            first = 16 * (q // 2) + 4 * (q % 2)
+            first = 32 * (q // 2) + 4 * (q % 2)
             nc.sync.dma_start(
-                planes[32 * q : 32 * q + 16, :].bitcast(I32), scales_x[first : first + 16, :].bitcast(I32)
+                planes[32 * q : 32 * q + GAP + 4, :].bitcast(I32), scales_x[first : first + GAP + 4, :].bitcast(I32)
             )
         late = []
-        for b in range(2):
-            late.append(held(f"w_late{b}", [P, PACK, P], F32, AT_SCALE_WIN + 2112 * b))
+        for b in range(BLOCKS):
+            late.append(placed(f"late{b}", [P, PACK, P], F32, AT_LATE + QUARTER * b))
             nc.sync.dma_start(
                 late[b][:], w1[P * PACK : K, b * P : (b + 1) * P].rearrange("(p j) c -> p j c", j=PACK)
             )
-        a_t = held("a_t", [P, D, CHUNKS], F32, AT_W0)
-        for i in range(CHUNKS):
-            nc.scalar.activation(a_t[:, :, i], e_t[:, :, i], ACT.Copy, scale=inv[:, i : i + 1])
-        a_rows = []
+        weights = keep.tile([P, D, PACK], F32, name="weights")
+        for j in range(PACK):
+            nc.scalar.activation(weights[:, :, j], exps[:, :, j], ACT.Copy, scale=inverse[:, j : j + 1])
+
+        def cast(grouped, rows):
+            nc.scalar.copy(grouped[:], rows.rearrange("p j c -> p c j"))
+            return grouped
+
+        grouped0 = cast(
+            placed("grouped0", [P, N, PACK], BF16, AT_GROUPED0), raw0[:].rearrange("p (j c) -> p j c", j=PACK)
+        )
+
+        spreads = []
         for d in range(D):
-            bank = psum.tile([P, CHUNKS, P], F32, name=f"spread{d}", tag=f"t{d}")
-            for i in range(CHUNKS):
-                nc.tensor.transpose(bank[:, i, :], a_t[:, d, i : i + 1].to_broadcast([P, P]), ident[:])
-            row = keep.tile([P, P, PACK], F32, name=f"a_row{d}")
-            nc.scalar.copy(row[:], bank[:].rearrange("m j p -> m p j"))
-            a_rows.append(row[:].rearrange("m p j -> m (p j)"))
+            bank = psum.tile([P, PACK, P], F32, name=f"spread{d}", tag=("acc1_2", "spare0", "spare1")[d])
+            for j in range(PACK):
+                nc.tensor.transpose(bank[:, j, :], weights[:, d, j : j + 1].to_broadcast([P, P]), ident[:])
+            spreads.append(bank)
+        weight_rows = []
+
+        def copy_row(d, row):
+            nc.scalar.copy(row[:], spreads[d][:].rearrange("m j p -> m p j"))
+            weight_rows.append(row[:].rearrange("m p j -> m (p j)"))
+
+        for d in range(2):
+            copy_row(d, keep.tile([P, P, PACK], F32, name=f"weight_row{d}"))
 
         def gather_words(z, lo, hi, piece):
-            nc.vector.tensor_copy(piece, word_win[z][:].bitcast(U32).indirect(offs_t[:, lo // 16 : hi // 16]))
-            return piece
+            nc.vector.tensor_copy(piece[:], word_window[z][:].bitcast(U32).indirect(offs_t[:, lo // 16 : hi // 16]))
+            return piece[:]
 
-        def quantize(n, grouped, at):
+        def quantize(name, grouped):
             width = grouped.shape[1]
-            codes = held(f"codes_w{n}", [P, width], U32, at)
-            scales = keep.tile([P, width], U8, name=f"scales_w{n}", align_bytes=64)
+            codes = keep.tile([P, width], U32, name=f"codes_{name}", align_bytes=64)
+            scales = keep.tile([P, width], U8, name=f"scales_{name}", align_bytes=64)
             nc.vector.quantize_mx(
                 out=codes[:].bitcast(FP8X4), scales=scales[:], in_=grouped[:].rearrange("p c j -> p (c j)")
             )
             return [(codes[:, c : c + P], scales[:, c : c + P]) for c in range(0, width, P)]
 
-        def one_pass(acc, weights, codes, z, lo, hi, start, stop):
-            nc.tensor.matmul_mx(
-                out=acc,
-                lhsT=weights[0].bitcast(FP8X4),
-                lhsT_scale=weights[1],
-                rhs=codes.bitcast(FP8X4),
-                rhs_scale=planes[8 * z : P, lo:hi],
-                start=start,
-                stop=stop,
-            )
-
-        cut = S - PIECE
-        stretches = [(0, BANK), (BANK, cut), (cut, S)]
-        tags = [["acc0_0", "acc0_1", "acc0_2"], ["acc1_0", "acc1_1", "t2"]]
+        pieces = [(0, BANK), (BANK, S - PIECE), (S - PIECE, S)]
         acc = [
-            [psum.tile([P, hi - lo], F32, name=f"acc{b}_{lo}", tag=tag) for tag, (lo, hi) in zip(tags[b], stretches)]
-            for b in range(2)
+            [psum.tile([P, hi - lo], F32, name=f"acc{b}_{i}", tag=f"acc{b}_{i}") for i, (lo, hi) in enumerate(pieces)]
+            for b in range(BLOCKS)
         ]
 
-        w0 = quantize(0, grouped0, AT_CODES_W0)
-        codes_x0 = gather_words(0, 0, S, keep.tile([P, S], U32, name="codes_x0", align_bytes=64)[:])
-        for b in range(2):
-            for bank, (lo, hi) in zip(acc[b], stretches):
-                one_pass(bank[:], w0[b], codes_x0[:, lo:hi], 0, lo, hi, True, False)
+        codes_x0 = gather_words(0, 0, S, keep.tile([P, S], U32, name="codes_x0", align_bytes=64))
+        w_pass0 = quantize("w0", grouped0)
+        grouped1 = [
+            cast(keep.tile([P, P, PACK], BF16, name=f"grouped1{b}", align_bytes=64), late[b][:])
+            for b in range(BLOCKS)
+        ]
+        copy_row(2, placed("weight_row2", [P, P, PACK], F32, AT_ROW2))
+        codes_x1 = [
+            gather_words(1, *pieces[0], placed("codes_x1_0", [P, BANK], U32, AT_RAW0)),
+            gather_words(1, *pieces[1], placed("codes_x1_1", [P, PIECE], U32, AT_RAW0 + 4 * BANK)),
+        ]
+        w_pass1 = quantize("w10", grouped1[0])
+        codes_x1.append(gather_words(1, *pieces[2], placed("codes_x1_2", [P, PIECE], U32, AT_LATE)))
+        w_pass1 = w_pass1 + quantize("w11", grouped1[1])
+        y = [keep.tile([P, S], F32, name=f"y{b}") for b in range(BLOCKS)]
 
-        grouped = [cast(f"grouped1{b}", late[b][:].rearrange("p j c -> p c j"), AT_GROUPED1 + 1024 * b) for b in range(2)]
-        codes_x1 = [gather_words(1, 0, BANK, keep.tile([P, BANK], U32, name="codes_x1_0", align_bytes=64)[:])]
-        w1q = quantize(1, grouped[0], AT_CODES_W1)
-        codes_x1.append(gather_words(1, BANK, cut, held("codes_x1_1", [P, PIECE], U32, AT_SCALE_WIN)[:]))
-        w1q = w1q + quantize(2, grouped[1], AT_CODES_W1 + 512)
-        codes_x1.append(gather_words(1, cut, S, held("codes_x1_2", [P, PIECE], U32, AT_SCALE_WIN + 2112)[:]))
-        y = [keep.tile([P, S], F32, name=f"y{b}") for b in range(2)]
-        for b, i in ((0, 0), (0, 1), (0, 2), (1, 0), (1, 1), (1, 2)):
-            one_pass(acc[b][i][:], w1q[b], codes_x1[i], 1, *stretches[i], False, True)
-        for b, i in ((0, 0), (0, 1), (0, 2), (1, 0), (1, 1), (1, 2)):
-            lo, hi = stretches[i]
-            copy = nc.vector.tensor_copy if (b, i) == (0, 2) else nc.scalar.copy
-            copy(y[b][:, lo:hi], acc[b][i][:])
-        a_col = keep.tile([P, 2, CHUNKS], F32, name="a_col")
+        for z, w_pass in enumerate((w_pass0, w_pass1)):
+            for b in range(BLOCKS):
+                for i, (lo, hi) in enumerate(pieces):
+                    nc.tensor.matmul_mx(
+                        out=acc[b][i][:],
+                        lhsT=w_pass[b][0].bitcast(FP8X4),
+                        lhsT_scale=w_pass[b][1],
+                        rhs=(codes_x0[:, lo:hi] if z == 0 else codes_x1[i]).bitcast(FP8X4),
+                        rhs_scale=planes[GAP * z : P, lo:hi],
+                        start=(z == 0),
+                        stop=(z == PASSES - 1),
+                    )
+
+        def copy_out(b, i):
+            lo, hi = pieces[i]
+            (nc.scalar.copy if i == 0 else nc.vector.tensor_copy)(y[b][:, lo:hi], acc[b][i][:])
+
+        for i in range(len(pieces)):
+            copy_out(0, i)
+        copy_out(1, 0)
+
+        weight_columns = keep.tile([P, 2, CHUNKS], F32, name="weight_columns")
         for d in range(2):
             bank = psum.tile([P, CHUNKS, P], F32, name=f"column{d}", tag=f"acc{d}_0")
-            for i in range(CHUNKS):
-                nc.tensor.transpose(bank[:, i, :], a_rows[d][:, i * P : (i + 1) * P], ident[:])
-            nc.scalar.copy(a_col[:, d, :], bank[:, :, 0])
+            for c in range(CHUNKS):
+                nc.tensor.transpose(bank[:, c, :], weight_rows[d][:, c * P : (c + 1) * P], ident[:])
+            nc.scalar.copy(weight_columns[:, d, :], bank[:, :, 0])
 
         def weighted(b, d):
-            h = keep.tile([P, V], F32, name=f"h{b}{d}")
-            nc.vector.tensor_tensor(h[:], y[b][:].indirect(pos_t[d][:]), a_rows[d], ALU.mult)
-            return h
+            product = keep.tile([P, V], F32, name=f"product{b}{d}")
+            nc.vector.tensor_tensor(product[:], y[b][:].indirect(pos_t[d][:]), weight_rows[d], ALU.mult)
+            return product
 
-        def plain(b, d):
-            g = held(f"g{b}{d}", [P, V], F32, AT_Y1 + 4 * V * (d % 2))
-            nc.scalar.activation(g[:], y[b][:].indirect(pos_t[d][:]), ACT.Copy)
-            return g
+        def fetched(b, d):
+            columns = keep.tile([P, V], F32, name=f"columns{b}{d}")
+            nc.scalar.activation(columns[:], y[b][:].indirect(pos_t[d][:]), ACT.Copy)
+            return columns
 
-        h00 = weighted(0, 0)
-        h01 = weighted(0, 1)
-        h12 = weighted(1, 2)
+        product02 = weighted(0, 2)
+        copy_out(1, 1)
+        copy_out(1, 2)
+        product10 = weighted(1, 0)
+        product11 = weighted(1, 1)
         turned = []
         for d in range(2):
-            g = plain(1, d)
-            bank = psum.tile([P, CHUNKS, P], F32, name=f"turned{d}", tag=f"t{d}")
-            for i in range(CHUNKS):
-                nc.tensor.transpose(bank[:, i, :], g[:, i * P : (i + 1) * P], ident[:])
+            columns = fetched(0, d)
+            bank = psum.tile([P, CHUNKS, P], F32, name=f"turned{d}", tag=("acc0_2", "spare0")[d])
+            for c in range(CHUNKS):
+                nc.tensor.transpose(bank[:, c, :], columns[:, c * P : (c + 1) * P], ident[:])
             turned.append(bank)
-        g02 = plain(0, 2)
-        half = V // 2
+        columns12 = fetched(1, 2)
+
         back = [psum.tile([P, 2, P], F32, name=f"back{u}", tag=f"acc{u}_1") for u in range(2)]
         for u in range(2):
             for d in range(2):
                 scaled = keep.tile([P, 2, P], F32, name=f"scaled{u}{d}")
                 for i in range(2):
                     c = 2 * u + i
-                    nc.scalar.activation(scaled[:, i, :], turned[d][:, c, :], ACT.Copy, scale=a_col[:, d, c : c + 1])
+                    nc.scalar.activation(
+                        scaled[:, i, :], turned[d][:, c, :], ACT.Copy, scale=weight_columns[:, d, c : c + 1]
+                    )
                 for i in range(2):
                     nc.tensor.matmul(
                         back[u][:, i, :], scaled[:, i, :], ident[:], is_transpose=True,
                         start=(d == 0 and i == 0), stop=(d == 1 and i == 1),
                     )
 
-        def finish_block1(u):
-            cols = slice(u * half, (u + 1) * half)
-            out1 = keep.tile([P, half], F32, name=f"out1_{u}")
-            nc.vector.tensor_tensor(out1[:], back[u][:].rearrange("m i v -> m (i v)"), h12[:, cols], ALU.add)
-            nc.sync.dma_start(out[P : 2 * P, cols], out1[:])
-
+        halves = [slice(u * HALF, (u + 1) * HALF) for u in range(2)]
+        product12 = keep.tile([P, V], F32, name="product12")
+        nc.vector.tensor_tensor(product12[:], columns12[:], weight_rows[2], ALU.mult)
         part = keep.tile([P, V], F32, name="part")
-        nc.vector.tensor_tensor(part[:], h00[:], h01[:], ALU.add)
-        h02 = keep.tile([P, V], F32, name="h02")
-        nc.vector.tensor_tensor(h02[:], g02[:], a_rows[2], ALU.mult)
-        out0 = keep.tile([P, V], F32, name="out0")
-        nc.vector.tensor_tensor(out0[:], part[:], h02[:], ALU.add)
-        nc.sync.dma_start(out[0:P, :], out0[:])
-        finish_block1(0)
-        finish_block1(1)
+        for cols in halves:
+            nc.vector.tensor_tensor(part[:, cols], product10[:, cols], product11[:, cols], ALU.add)
+        for u, cols in enumerate(halves):
+            result = keep.tile([P, HALF], F32, name=f"result1{u}")
+            nc.vector.tensor_tensor(result[:], part[:, cols], product12[:, cols], ALU.add)
+            nc.sync.dma_start(out[P:N, cols], result[:])
+        for u, cols in enumerate(halves):
+            result = keep.tile([P, HALF], F32, name=f"result0{u}")
+            nc.vector.tensor_tensor(result[:], back[u][:].rearrange("m i v -> m (i v)"), product02[:, cols], ALU.add)
+            nc.sync.dma_start(out[0:P, cols], result[:])

@@ -26,7 +26,6 @@ CHUNKS = V // P
 HALF = V // 2
 PIECE = 256
 GAP = 12
-CLEARED_BY_GPSIMD = 3 * T // 4
 
 QUARTER = 4 * PACK * P
 AT_LATE = 0
@@ -53,8 +52,8 @@ def tile_picked_gatv_none_p_kernel(
         pos_t = [lists.tile([P, V // 16], U16, name=f"pos_t{d}") for d in range(D)]
 
         scale_window = placed("scale_window", [P, T], U8, AT_SCALE_WINDOW)
-        nc.gpsimd.memset(scale_window[:, 0:CLEARED_BY_GPSIMD].bitcast(I32), 0)
-        nc.vector.memset(scale_window[:, CLEARED_BY_GPSIMD:T].bitcast(I32), 0)
+        nc.vector.memset(scale_window[32:64, :].bitcast(I32), 0)
+        nc.vector.memset(scale_window[64:P, :].bitcast(I32), 0)
         planes = keep.tile([P, S], U8, name="planes", align_bytes=64)
         nc.gpsimd.memset(planes[:].bitcast(I32), 0)
         ident = keep.tile([P, P], F32, name="ident")
@@ -64,13 +63,9 @@ def tile_picked_gatv_none_p_kernel(
         scores = score_tile[:, :, 0:PACK]
         nc.sync.dma_start(scores, score[:, 0, :].rearrange("d (p j) -> p d j", j=PACK))
         nc.sync.dma_start(offs_t[:], offs)
-        nc.sync.dma_start(pos_t[0][:], pos1)
-        for h in range(2):
-            for z in range(PASSES):
-                first = 32 * h + GAP * z
-                (nc.scalar if (h, z) == (1, PASSES - 1) else nc.sync).dma_start(
-                    scale_window[first : first + 8, :].bitcast(I32), x_scales[z, 8 * h : 8 * h + 8, :].bitcast(I32)
-                )
+        scale_loads = ((nc.sync, 0, 0, 16, 0), (nc.sync, 1, 4, 12, 16), (nc.scalar, 1, 12, 16, 24), (nc.scalar, 1, 0, 4, 28))
+        for queue, z, lo, hi, first in scale_loads:
+            queue.dma_start(scale_window[first : first + hi - lo, :].bitcast(I32), x_scales[z, lo:hi, :].bitcast(I32))
         word_window = [keep.tile([P, T], I32, name=f"word_window{z}", align_bytes=64) for z in range(PASSES)]
 
         def load_words(z):
@@ -79,9 +74,9 @@ def tile_picked_gatv_none_p_kernel(
         load_words(0)
         raw0 = placed("raw0", [P, PACK * N], F32, AT_RAW0)
         nc.sync.dma_start(raw0[:], w1[0 : P * PACK, :].rearrange("(p j) c -> p (j c)", j=PACK))
-        nc.sync.dma_start(pos_t[1][:], pos2)
+        for d, pos in enumerate((pos1, pos2, pos3)):
+            nc.sync.dma_start(pos_t[d][:], pos)
         load_words(1)
-        nc.sync.dma_start(pos_t[2][:], pos3)
 
         neg_scores = keep.tile([P, D, PACK], F32, name="neg_scores")
         nc.scalar.activation(neg_scores[:], scores, ACT.Copy, scale=-1.0)
@@ -103,11 +98,14 @@ def tile_picked_gatv_none_p_kernel(
         nc.scalar.activation(root[:], total[:], ACT.Abs_reciprocal_sqrt)
         inverse = keep.tile([P, PACK], F32, name="inverse")
         nc.scalar.activation(inverse[:], root[:], ACT.Square)
-        for q in range(4):
-            first = 32 * (q // 2) + 4 * (q % 2)
-            nc.sync.dma_start(
-                planes[32 * q : 32 * q + GAP + 4, :].bitcast(I32), scales_x[first : first + GAP + 4, :].bitcast(I32)
-            )
+
+        def move_rows(to, first, count):
+            nc.sync.dma_start(planes[to : to + count, :].bitcast(I32), scales_x[first : first + count, :].bitcast(I32))
+
+        for q in range(1, 4):
+            move_rows(32 * q, 4 * q, GAP + 4)
+        move_rows(0, 0, 4)
+        move_rows(GAP, 28, 4)
         late = []
         for b in range(BLOCKS):
             late.append(placed(f"late{b}", [P, PACK, P], F32, AT_LATE + QUARTER * b))

@@ -1,7 +1,6 @@
 from contextlib import ExitStack
 
 import concourse.mybir as mybir
-from concourse.masks import make_identity
 
 K, T, S, D, V, N = 1024, 2048, 1024, 3, 512, 256
 FLOPS = 2 * K * N * S
@@ -18,21 +17,23 @@ ALU = mybir.AluOpType
 ACT = mybir.ActivationFunctionType
 
 P = 128
+QUAD = 32
 PACK = 4
 PASSES = K // (P * PACK)
 BLOCKS = N // P
-BANK = 512
 CHUNKS = V // P
 HALF = V // 2
+BANK = 512
 PIECE = 256
 GAP = 12
 
 QUARTER = 4 * PACK * P
-AT_LATE = 0
-AT_SCALE_WINDOW = AT_LATE + QUARTER // 2
-AT_ROW2 = AT_LATE + 3 * QUARTER // 2
-AT_GROUPED0 = AT_ROW2 + 4 * V
-AT_RAW0 = AT_GROUPED0 + 2 * PACK * N
+AT_ROWS = 0
+AT_RAW0 = 2 * V
+AT_PLANES = 4 * V * D
+AT_LATE = AT_PLANES + S
+AT_TOTAL = AT_LATE + QUARTER - 64
+AT_GROUPED0 = AT_LATE + 2 * QUARTER
 
 
 def tile_picked_gatv_none_p_kernel(
@@ -51,97 +52,88 @@ def tile_picked_gatv_none_p_kernel(
         offs_t = lists.tile([P, S // 16], U16, name="offs_t")
         pos_t = [lists.tile([P, V // 16], U16, name=f"pos_t{d}") for d in range(D)]
 
-        scale_window = placed("scale_window", [P, T], U8, AT_SCALE_WINDOW)
-        nc.vector.memset(scale_window[32:64, :].bitcast(I32), 0)
-        nc.vector.memset(scale_window[64:P, :].bitcast(I32), 0)
-        planes = keep.tile([P, S], U8, name="planes", align_bytes=64)
-        nc.gpsimd.memset(planes[:].bitcast(I32), 0)
-        ident = keep.tile([P, P], F32, name="ident")
-        make_identity(nc, ident[:])
+        scale_window = keep.tile([P, T], U8, name="scale_window", align_bytes=64)
+        nc.gpsimd.memset(scale_window[QUAD : 2 * QUAD, :].bitcast(I32), 0)
+        nc.gpsimd.memset(scale_window[2 * QUAD : P, :].bitcast(I32), 0)
 
+        ident = keep.tile([P, P], F32, name="ident")
+        nc.vector.memset(ident[:], 0.0)
+        ones = keep.tile([P, QUAD], F32, name="ones")
+        nc.vector.memset(ones[:], 1.0)
+        column = keep.tile([P, QUAD], F32, name="column", align_bytes=64)
+        nc.vector.tensor_tensor_scan(column[:], ones[:], ones[:], 0.0, ALU.mult, ALU.add)
+        row = keep.tile([P, QUAD], F32, name="row", align_bytes=64)
+        nc.vector.transpose(row[:], column[:])
+        for q in range(P // QUAD):
+            part = slice(QUAD * q, QUAD * (q + 1))
+            nc.vector.tensor_tensor(ident[part, part], column[part, :], row[part, :], ALU.is_equal)
+
+        nc.sync.dma_start(offs_t[:], offs)
         score_tile = keep.tile([P, D, 2 * PACK], F32, name="score_tile")
         scores = score_tile[:, :, 0:PACK]
-        nc.sync.dma_start(scores, score[:, 0, :].rearrange("d (p j) -> p d j", j=PACK))
-        nc.sync.dma_start(offs_t[:], offs)
-        scale_loads = ((nc.sync, 0, 0, 16, 0), (nc.sync, 1, 4, 12, 16), (nc.scalar, 1, 12, 16, 24), (nc.scalar, 1, 0, 4, 28))
+        nc.scalar.dma_start(scores, score[:, 0, :].rearrange("d (p j) -> p d j", j=PACK))
+        scale_loads = ((nc.sync, 0, 0, 16, 0), (nc.sync, 1, 4, 12, 16), (nc.sync, 1, 12, 16, 24), (nc.scalar, 1, 0, 4, 28))
         for queue, z, lo, hi, first in scale_loads:
             queue.dma_start(scale_window[first : first + hi - lo, :].bitcast(I32), x_scales[z, lo:hi, :].bitcast(I32))
-        word_window = [keep.tile([P, T], I32, name=f"word_window{z}", align_bytes=64) for z in range(PASSES)]
 
         def load_words(z):
-            nc.sync.dma_start(word_window[z][:], x_words[z].rearrange("p c r -> p (c r)").bitcast(I32))
+            window = keep.tile([P, T], I32, name=f"window{z}", align_bytes=64)
+            nc.sync.dma_start(window[:], x_words[z].rearrange("p c r -> p (c r)").bitcast(I32))
+            return window
 
-        load_words(0)
-        raw0 = placed("raw0", [P, PACK * N], F32, AT_RAW0)
-        nc.sync.dma_start(raw0[:], w1[0 : P * PACK, :].rearrange("(p j) c -> p (j c)", j=PACK))
+        window0 = load_words(0)
         for d, pos in enumerate((pos1, pos2, pos3)):
             nc.sync.dma_start(pos_t[d][:], pos)
-        load_words(1)
-
-        neg_scores = keep.tile([P, D, PACK], F32, name="neg_scores")
-        nc.scalar.activation(neg_scores[:], scores, ACT.Copy, scale=-1.0)
-        neg_max = keep.tile([P, PACK], F32, name="neg_max")
-        nc.vector.tensor_reduce(
-            neg_max[:], scores.rearrange("p d j -> p j d"), mybir.AxisListType.X, ALU.max, negate=True
+        raw0 = placed("raw0", [P, PACK, N], F32, AT_RAW0)
+        nc.sync.dma_start(
+            raw0[:].rearrange("p j c -> p (j c)"), w1[0 : P * PACK, :].rearrange("(p j) c -> p (j c)", j=PACK)
         )
-        exps = placed("exps", [P, D, PACK], F32, AT_GROUPED0)
-        total = keep.tile([P, PACK], F32, name="total")
+        window1 = load_words(1)
+
+        neg_scores = placed("neg_scores", [P, D, PACK], F32, AT_PLANES)
+        nc.scalar.activation(neg_scores[:], scores, ACT.Copy, scale=-1.0)
+        neg_top = keep.tile([P, PACK], F32, name="neg_top")
+        for j in range(PACK):
+            first, second, third = (neg_scores[:, d, j : j + 1] for d in range(D))
+            nc.gpsimd.tensor_scalar(neg_top[:, j : j + 1], first, second, third, ALU.min, ALU.min)
+        exps = keep.tile([P, D, PACK], F32, name="exps")
+        total_tile = placed("total", [P, 32], F32, AT_TOTAL)
+        total = total_tile[:, 0:PACK]
         for j in range(PACK):
             nc.scalar.activation(
-                exps[:, :, j], neg_scores[:, :, j], ACT.Exp, scale=-1.0, bias=neg_max[:, j : j + 1],
+                exps[:, :, j], neg_scores[:, :, j], ACT.Exp, scale=-1.0, bias=neg_top[:, j : j + 1],
                 accum_out=total[:, j : j + 1],
             )
+        planes = placed("planes", [P, S], U8, AT_PLANES)
+        nc.gpsimd.memset(planes[:].bitcast(I32), 0)
 
         scales_x = keep.tile([P, S], U8, name="scales_x", align_bytes=64)
         nc.vector.tensor_copy(scales_x[:], scale_window[:].indirect(offs_t[:]))
-        root = keep.tile([P, PACK], F32, name="root")
-        nc.scalar.activation(root[:], total[:], ACT.Abs_reciprocal_sqrt)
-        inverse = keep.tile([P, PACK], F32, name="inverse")
-        nc.scalar.activation(inverse[:], root[:], ACT.Square)
 
-        def move_rows(to, first, count):
-            nc.sync.dma_start(planes[to : to + count, :].bitcast(I32), scales_x[first : first + count, :].bitcast(I32))
+        def move_rows(queue, to, first, count):
+            queue.dma_start(planes[to : to + count, :].bitcast(I32), scales_x[first : first + count, :].bitcast(I32))
 
         for q in range(1, 4):
-            move_rows(32 * q, 4 * q, GAP + 4)
-        move_rows(0, 0, 4)
-        move_rows(GAP, 28, 4)
+            move_rows(nc.sync, QUAD * q, 4 * q, GAP + 4)
+        move_rows(nc.scalar, 0, 0, 4)
+        move_rows(nc.scalar, GAP, 28, 4)
+
+        minus_one = keep.tile([P, PACK], F32, name="minus_one")
+        nc.gpsimd.memset(minus_one[:], -1.0)
+        inverse = placed("inverse", [P, PACK], F32, AT_GROUPED0)
+        nc.gpsimd.tensor_tensor(inverse[:], total, minus_one[:], ALU.pow)
+        shares = keep.tile([P, D, PACK], F32, name="shares")
+        nc.gpsimd.tensor_tensor(shares[:], exps[:], inverse[:].unsqueeze(1).to_broadcast([P, D, PACK]), ALU.mult)
+
         late = []
         for b in range(BLOCKS):
             late.append(placed(f"late{b}", [P, PACK, P], F32, AT_LATE + QUARTER * b))
             nc.sync.dma_start(
                 late[b][:], w1[P * PACK : K, b * P : (b + 1) * P].rearrange("(p j) c -> p j c", j=PACK)
             )
-        weights = keep.tile([P, D, PACK], F32, name="weights")
-        for j in range(PACK):
-            nc.scalar.activation(weights[:, :, j], exps[:, :, j], ACT.Copy, scale=inverse[:, j : j + 1])
 
-        def cast(grouped, rows):
-            nc.scalar.copy(grouped[:], rows.rearrange("p j c -> p c j"))
-            return grouped
-
-        grouped0 = cast(
-            placed("grouped0", [P, N, PACK], BF16, AT_GROUPED0), raw0[:].rearrange("p (j c) -> p j c", j=PACK)
-        )
-
-        spreads = []
-        for d in range(D):
-            bank = psum.tile([P, PACK, P], F32, name=f"spread{d}", tag=("acc1_2", "spare0", "spare1")[d])
-            for j in range(PACK):
-                nc.tensor.transpose(bank[:, j, :], weights[:, d, j : j + 1].to_broadcast([P, P]), ident[:])
-            spreads.append(bank)
-        weight_rows = []
-
-        def copy_row(d, row):
-            nc.scalar.copy(row[:], spreads[d][:].rearrange("m j p -> m p j"))
-            weight_rows.append(row[:].rearrange("m p j -> m (p j)"))
-
-        for d in range(2):
-            copy_row(d, keep.tile([P, P, PACK], F32, name=f"weight_row{d}"))
-
-        def gather_words(z, lo, hi, piece):
-            nc.vector.tensor_copy(piece[:], word_window[z][:].bitcast(U32).indirect(offs_t[:, lo // 16 : hi // 16]))
-            return piece[:]
+        def cast(engine, grouped, rows):
+            engine(grouped, rows.rearrange("p j c -> p c j"))
 
         def quantize(name, grouped):
             width = grouped.shape[1]
@@ -152,59 +144,88 @@ def tile_picked_gatv_none_p_kernel(
             )
             return [(codes[:, c : c + P], scales[:, c : c + P]) for c in range(0, width, P)]
 
+        grouped0 = placed("grouped0", [P, N, PACK], BF16, AT_GROUPED0)
+        cast(nc.scalar.copy, grouped0[:, 0:P, :], raw0[:, :, 0:P])
+        cast(nc.gpsimd.tensor_copy, grouped0[:, P:N, :], raw0[:, :, P:N])
+
+        spreads = []
+        for d in range(D):
+            bank = psum.tile([P, PACK, P], F32, name=f"spread{d}", tag=("acc1_2", "spare0", "spare1")[d])
+            for j in range(PACK):
+                nc.tensor.transpose(bank[:, j, :], shares[:, d, j : j + 1].to_broadcast([P, P]), ident[:])
+            spreads.append(bank)
+        share_rows = []
+        for d in range(D):
+            tile = placed(f"share_row{d}", [P, P, PACK], F32, AT_ROWS + 4 * V * d)
+            nc.scalar.copy(tile[:], spreads[d][:].rearrange("m j p -> m p j"))
+            share_rows.append(tile[:].rearrange("m p j -> m (p j)"))
+
+        def gather_words(piece, window, lo, hi):
+            nc.vector.tensor_copy(piece[:], window[:].bitcast(U32).indirect(offs_t[:, lo // 16 : hi // 16]))
+            return piece[:]
+
         pieces = [(0, BANK), (BANK, S - PIECE), (S - PIECE, S)]
         acc = [
             [psum.tile([P, hi - lo], F32, name=f"acc{b}_{i}", tag=f"acc{b}_{i}") for i, (lo, hi) in enumerate(pieces)]
             for b in range(BLOCKS)
         ]
-
-        codes_x0 = gather_words(0, 0, S, keep.tile([P, S], U32, name="codes_x0", align_bytes=64))
+        codes_x0 = gather_words(keep.tile([P, S], U32, name="codes_x0", align_bytes=64), window0, 0, S)
         w_pass0 = quantize("w0", grouped0)
-        grouped1 = [
-            cast(keep.tile([P, P, PACK], BF16, name=f"grouped1{b}", align_bytes=64), late[b][:])
-            for b in range(BLOCKS)
+        grouped1 = [keep.tile([P, P, PACK], BF16, name=f"grouped1{b}", align_bytes=64) for b in range(BLOCKS)]
+        for b in range(BLOCKS):
+            cast(nc.scalar.copy, grouped1[b][:], late[b][:])
+        words1 = [
+            gather_words(keep.tile([P, hi - lo], U32, name=f"codes_x1_{lo}", align_bytes=64), window1, lo, hi)
+            for lo, hi in pieces[:-1]
         ]
-        copy_row(2, placed("weight_row2", [P, P, PACK], F32, AT_ROW2))
-        codes_x1 = [
-            gather_words(1, *pieces[0], placed("codes_x1_0", [P, BANK], U32, AT_RAW0)),
-            gather_words(1, *pieces[1], placed("codes_x1_1", [P, PIECE], U32, AT_RAW0 + 4 * BANK)),
-        ]
-        w_pass1 = quantize("w10", grouped1[0])
-        codes_x1.append(gather_words(1, *pieces[2], placed("codes_x1_2", [P, PIECE], U32, AT_LATE)))
-        w_pass1 = w_pass1 + quantize("w11", grouped1[1])
+        w_pass1 = quantize("w10", grouped1[0]) + quantize("w11", grouped1[1])
+        last = placed("codes_x1_last", [P, PIECE], U32, AT_LATE + QUARTER + QUARTER // 4)
+        words1.append(gather_words(last, window1, *pieces[-1]))
         y = [keep.tile([P, S], F32, name=f"y{b}") for b in range(BLOCKS)]
 
-        for z, w_pass in enumerate((w_pass0, w_pass1)):
-            for b in range(BLOCKS):
-                for i, (lo, hi) in enumerate(pieces):
-                    nc.tensor.matmul_mx(
-                        out=acc[b][i][:],
-                        lhsT=w_pass[b][0].bitcast(FP8X4),
-                        lhsT_scale=w_pass[b][1],
-                        rhs=(codes_x0[:, lo:hi] if z == 0 else codes_x1[i]).bitcast(FP8X4),
-                        rhs_scale=planes[GAP * z : P, lo:hi],
-                        start=(z == 0),
-                        stop=(z == PASSES - 1),
-                    )
-
-        def copy_out(b, i):
+        def multiply(z, b, i):
             lo, hi = pieces[i]
-            (nc.scalar.copy if i == 0 else nc.vector.tensor_copy)(y[b][:, lo:hi], acc[b][i][:])
+            codes, scales = (w_pass0, w_pass1)[z][b]
+            nc.tensor.matmul_mx(
+                out=acc[b][i][:],
+                lhsT=codes.bitcast(FP8X4),
+                lhsT_scale=scales,
+                rhs=(codes_x0[:, lo:hi] if z == 0 else words1[i]).bitcast(FP8X4),
+                rhs_scale=planes[GAP * z : P, lo:hi],
+                start=(z == 0),
+                stop=(z == PASSES - 1),
+            )
 
+        def copy_out(engine, b, i):
+            lo, hi = pieces[i]
+            engine(y[b][:, lo:hi], acc[b][i][:])
+
+        for b in range(BLOCKS):
+            for i in range(len(pieces)):
+                multiply(0, b, i)
+        for b in range(BLOCKS):
+            for i in range(len(pieces) - 1):
+                multiply(1, b, i)
+        for b in range(BLOCKS):
+            multiply(1, b, len(pieces) - 1)
+        copy_out(nc.scalar.copy, 0, 0)
+        for i in range(1, len(pieces)):
+            copy_out(nc.vector.tensor_copy, 0, i)
         for i in range(len(pieces)):
-            copy_out(0, i)
-        copy_out(1, 0)
+            copy_out(nc.scalar.copy, 1, i)
 
-        weight_columns = keep.tile([P, 2, CHUNKS], F32, name="weight_columns")
+        share_columns = keep.tile([P, 2, CHUNKS], F32, name="share_columns")
         for d in range(2):
-            bank = psum.tile([P, CHUNKS, P], F32, name=f"column{d}", tag=f"acc{d}_0")
+            bank = psum.tile([P, CHUNKS, P], F32, name=f"column{d}", tag=f"acc{d}_2")
             for c in range(CHUNKS):
-                nc.tensor.transpose(bank[:, c, :], weight_rows[d][:, c * P : (c + 1) * P], ident[:])
-            nc.scalar.copy(weight_columns[:, d, :], bank[:, :, 0])
+                nc.tensor.transpose(bank[:, c, :], share_rows[d][:, c * P : (c + 1) * P], ident[:])
+            nc.scalar.copy(share_columns[:, d, :], bank[:, :, 0])
 
-        def weighted(b, d):
-            product = keep.tile([P, V], F32, name=f"product{b}{d}")
-            nc.vector.tensor_tensor(product[:], y[b][:].indirect(pos_t[d][:]), weight_rows[d], ALU.mult)
+        def weighted(b, d, lo=0, hi=V):
+            name = f"product{b}{d}_{lo}"
+            product = placed(name, [P, hi - lo], F32, AT_ROWS) if lo else keep.tile([P, hi - lo], F32, name=name)
+            picked = y[b][:].indirect(pos_t[d][:, lo // 16 : hi // 16])
+            nc.vector.tensor_tensor(product[:], picked, share_rows[d][:, lo:hi], ALU.mult)
             return product
 
         def fetched(b, d):
@@ -212,28 +233,27 @@ def tile_picked_gatv_none_p_kernel(
             nc.scalar.activation(columns[:], y[b][:].indirect(pos_t[d][:]), ACT.Copy)
             return columns
 
-        product02 = weighted(0, 2)
-        copy_out(1, 1)
-        copy_out(1, 2)
+        product02 = [weighted(0, 2, 0, HALF)]
         product10 = weighted(1, 0)
         product11 = weighted(1, 1)
+        product02.append(weighted(0, 2, HALF, V))
         turned = []
         for d in range(2):
             columns = fetched(0, d)
-            bank = psum.tile([P, CHUNKS, P], F32, name=f"turned{d}", tag=("acc0_2", "spare0")[d])
+            bank = psum.tile([P, CHUNKS, P], F32, name=f"turned{d}", tag=f"spare{d}")
             for c in range(CHUNKS):
                 nc.tensor.transpose(bank[:, c, :], columns[:, c * P : (c + 1) * P], ident[:])
             turned.append(bank)
         columns12 = fetched(1, 2)
 
-        back = [psum.tile([P, 2, P], F32, name=f"back{u}", tag=f"acc{u}_1") for u in range(2)]
+        back = [psum.tile([P, 2, P], F32, name=f"back{u}", tag=f"acc{u}_0") for u in range(2)]
         for u in range(2):
             for d in range(2):
                 scaled = keep.tile([P, 2, P], F32, name=f"scaled{u}{d}")
                 for i in range(2):
                     c = 2 * u + i
                     nc.scalar.activation(
-                        scaled[:, i, :], turned[d][:, c, :], ACT.Copy, scale=weight_columns[:, d, c : c + 1]
+                        scaled[:, i, :], turned[d][:, c, :], ACT.Copy, scale=share_columns[:, d, c : c + 1]
                     )
                 for i in range(2):
                     nc.tensor.matmul(
@@ -242,16 +262,16 @@ def tile_picked_gatv_none_p_kernel(
                     )
 
         halves = [slice(u * HALF, (u + 1) * HALF) for u in range(2)]
-        product12 = keep.tile([P, V], F32, name="product12")
-        nc.vector.tensor_tensor(product12[:], columns12[:], weight_rows[2], ALU.mult)
         part = keep.tile([P, V], F32, name="part")
         for cols in halves:
             nc.vector.tensor_tensor(part[:, cols], product10[:, cols], product11[:, cols], ALU.add)
+        product12 = keep.tile([P, V], F32, name="product12")
+        nc.vector.tensor_tensor(product12[:], columns12[:], share_rows[2], ALU.mult)
         for u, cols in enumerate(halves):
             result = keep.tile([P, HALF], F32, name=f"result1{u}")
             nc.vector.tensor_tensor(result[:], part[:, cols], product12[:, cols], ALU.add)
             nc.sync.dma_start(out[P:N, cols], result[:])
         for u, cols in enumerate(halves):
             result = keep.tile([P, HALF], F32, name=f"result0{u}")
-            nc.vector.tensor_tensor(result[:], back[u][:].rearrange("m i v -> m (i v)"), product02[:, cols], ALU.add)
+            nc.vector.tensor_tensor(result[:], back[u][:].rearrange("m i v -> m (i v)"), product02[u][:], ALU.add)
             nc.sync.dma_start(out[0:P, cols], result[:])

@@ -30,10 +30,11 @@ GAP = 12
 QUARTER = 4 * PACK * P
 AT_ROWS = 0
 AT_RAW0 = 2 * V
-AT_PLANES = 4 * V * D
-AT_LATE = AT_PLANES + S
-AT_TOTAL = AT_LATE + QUARTER - 64
-AT_GROUPED0 = AT_LATE + 2 * QUARTER
+AT_LATE = 4 * V * 2 + 4 * V
+AT_SCALE_WINDOW = AT_LATE + QUARTER // 2
+AT_ROW2 = AT_LATE + 2 * QUARTER - 64
+AT_GROUPED0 = AT_ROW2 + 4 * V
+AT_SCALED = AT_GROUPED0 + 2 * PACK * N
 
 
 def tile_picked_gatv_none_p_kernel(
@@ -52,10 +53,12 @@ def tile_picked_gatv_none_p_kernel(
         offs_t = lists.tile([P, S // 16], U16, name="offs_t")
         pos_t = [lists.tile([P, V // 16], U16, name=f"pos_t{d}") for d in range(D)]
 
-        scale_window = keep.tile([P, T], U8, name="scale_window", align_bytes=64)
+        scale_window = placed("scale_window", [P, T], U8, AT_SCALE_WINDOW)
         nc.gpsimd.memset(scale_window[QUAD : 2 * QUAD, :].bitcast(I32), 0)
         nc.gpsimd.memset(scale_window[2 * QUAD : P, :].bitcast(I32), 0)
 
+        planes = keep.tile([P, S], U8, name="planes", align_bytes=64)
+        nc.gpsimd.memset(planes[:].bitcast(I32), 0)
         ident = keep.tile([P, P], F32, name="ident")
         nc.vector.memset(ident[:], 0.0)
         ones = keep.tile([P, QUAD], F32, name="ones")
@@ -68,44 +71,41 @@ def tile_picked_gatv_none_p_kernel(
             part = slice(QUAD * q, QUAD * (q + 1))
             nc.vector.tensor_tensor(ident[part, part], column[part, :], row[part, :], ALU.is_equal)
 
-        nc.sync.dma_start(offs_t[:], offs)
         score_tile = keep.tile([P, D, 2 * PACK], F32, name="score_tile")
         scores = score_tile[:, :, 0:PACK]
-        nc.scalar.dma_start(scores, score[:, 0, :].rearrange("d (p j) -> p d j", j=PACK))
-        scale_loads = ((nc.sync, 0, 0, 16, 0), (nc.sync, 1, 4, 12, 16), (nc.sync, 1, 12, 16, 24), (nc.scalar, 1, 0, 4, 28))
+        nc.sync.dma_start(scores, score[:, 0, :].rearrange("d (p j) -> p d j", j=PACK))
+        scale_loads = ((nc.sync, 0, 0, 16, 0), (nc.sync, 1, 4, 12, 16), (nc.scalar, 1, 12, 16, 24), (nc.scalar, 1, 0, 4, 28))
         for queue, z, lo, hi, first in scale_loads:
             queue.dma_start(scale_window[first : first + hi - lo, :].bitcast(I32), x_scales[z, lo:hi, :].bitcast(I32))
+        nc.sync.dma_start(offs_t[:], offs)
 
-        def load_words(z):
+        def load_words(z, cuts):
             window = keep.tile([P, T], I32, name=f"window{z}", align_bytes=64)
-            nc.sync.dma_start(window[:], x_words[z].rearrange("p c r -> p (c r)").bitcast(I32))
+            words = x_words[z].rearrange("p c r -> p (c r)").bitcast(I32)
+            for lo, hi in zip(cuts, cuts[1:]):
+                nc.sync.dma_start(window[:, lo:hi], words[:, lo:hi])
             return window
 
-        window0 = load_words(0)
-        for d, pos in enumerate((pos1, pos2, pos3)):
-            nc.sync.dma_start(pos_t[d][:], pos)
+        window0 = load_words(0, [0, T // 2, T])
         raw0 = placed("raw0", [P, PACK, N], F32, AT_RAW0)
         nc.sync.dma_start(
             raw0[:].rearrange("p j c -> p (j c)"), w1[0 : P * PACK, :].rearrange("(p j) c -> p (j c)", j=PACK)
         )
-        window1 = load_words(1)
+        window1 = load_words(1, [0, T])
 
-        neg_scores = placed("neg_scores", [P, D, PACK], F32, AT_PLANES)
+        neg_scores = keep.tile([P, D, PACK], F32, name="neg_scores")
         nc.scalar.activation(neg_scores[:], scores, ACT.Copy, scale=-1.0)
         neg_top = keep.tile([P, PACK], F32, name="neg_top")
-        for j in range(PACK):
-            first, second, third = (neg_scores[:, d, j : j + 1] for d in range(D))
-            nc.gpsimd.tensor_scalar(neg_top[:, j : j + 1], first, second, third, ALU.min, ALU.min)
-        exps = keep.tile([P, D, PACK], F32, name="exps")
-        total_tile = placed("total", [P, 32], F32, AT_TOTAL)
-        total = total_tile[:, 0:PACK]
+        nc.vector.tensor_reduce(
+            neg_top[:], scores.rearrange("p d j -> p j d"), mybir.AxisListType.X, ALU.max, negate=True
+        )
+        exps = placed("exps", [P, D, PACK], F32, AT_GROUPED0)
+        total = keep.tile([P, PACK], F32, name="total")
         for j in range(PACK):
             nc.scalar.activation(
                 exps[:, :, j], neg_scores[:, :, j], ACT.Exp, scale=-1.0, bias=neg_top[:, j : j + 1],
                 accum_out=total[:, j : j + 1],
             )
-        planes = placed("planes", [P, S], U8, AT_PLANES)
-        nc.gpsimd.memset(planes[:].bitcast(I32), 0)
 
         scales_x = keep.tile([P, S], U8, name="scales_x", align_bytes=64)
         nc.vector.tensor_copy(scales_x[:], scale_window[:].indirect(offs_t[:]))
@@ -115,15 +115,16 @@ def tile_picked_gatv_none_p_kernel(
 
         for q in range(1, 4):
             move_rows(nc.sync, QUAD * q, 4 * q, GAP + 4)
-        move_rows(nc.scalar, 0, 0, 4)
-        move_rows(nc.scalar, GAP, 28, 4)
+        move_rows(nc.sync, 0, 0, 4)
+        move_rows(nc.sync, GAP, 28, 4)
 
-        minus_one = keep.tile([P, PACK], F32, name="minus_one")
-        nc.gpsimd.memset(minus_one[:], -1.0)
-        inverse = placed("inverse", [P, PACK], F32, AT_GROUPED0)
-        nc.gpsimd.tensor_tensor(inverse[:], total, minus_one[:], ALU.pow)
+        root = keep.tile([P, PACK], F32, name="root")
+        nc.scalar.activation(root[:], total[:], ACT.Abs_reciprocal_sqrt)
+        inverse = keep.tile([P, PACK], F32, name="inverse")
+        nc.scalar.activation(inverse[:], root[:], ACT.Square)
         shares = keep.tile([P, D, PACK], F32, name="shares")
-        nc.gpsimd.tensor_tensor(shares[:], exps[:], inverse[:].unsqueeze(1).to_broadcast([P, D, PACK]), ALU.mult)
+        for j in range(PACK):
+            nc.scalar.activation(shares[:, :, j], exps[:, :, j], ACT.Copy, scale=inverse[:, j : j + 1])
 
         late = []
         for b in range(BLOCKS):
@@ -131,6 +132,9 @@ def tile_picked_gatv_none_p_kernel(
             nc.sync.dma_start(
                 late[b][:], w1[P * PACK : K, b * P : (b + 1) * P].rearrange("(p j) c -> p j c", j=PACK)
             )
+
+        for d, pos in enumerate((pos1, pos2, pos3)):
+            nc.sync.dma_start(pos_t[d][:], pos)
 
         def cast(engine, grouped, rows):
             engine(grouped, rows.rearrange("p j c -> p c j"))
@@ -145,8 +149,7 @@ def tile_picked_gatv_none_p_kernel(
             return [(codes[:, c : c + P], scales[:, c : c + P]) for c in range(0, width, P)]
 
         grouped0 = placed("grouped0", [P, N, PACK], BF16, AT_GROUPED0)
-        cast(nc.scalar.copy, grouped0[:, 0:P, :], raw0[:, :, 0:P])
-        cast(nc.gpsimd.tensor_copy, grouped0[:, P:N, :], raw0[:, :, P:N])
+        cast(nc.scalar.copy, grouped0[:], raw0[:])
 
         spreads = []
         for d in range(D):
@@ -155,10 +158,14 @@ def tile_picked_gatv_none_p_kernel(
                 nc.tensor.transpose(bank[:, j, :], shares[:, d, j : j + 1].to_broadcast([P, P]), ident[:])
             spreads.append(bank)
         share_rows = []
-        for d in range(D):
-            tile = placed(f"share_row{d}", [P, P, PACK], F32, AT_ROWS + 4 * V * d)
+
+        def copy_row(d, at):
+            tile = placed(f"share_row{d}", [P, P, PACK], F32, at)
             nc.scalar.copy(tile[:], spreads[d][:].rearrange("m j p -> m p j"))
             share_rows.append(tile[:].rearrange("m p j -> m (p j)"))
+
+        for d in range(2):
+            copy_row(d, AT_ROWS + 4 * V * d)
 
         def gather_words(piece, window, lo, hi):
             nc.vector.tensor_copy(piece[:], window[:].bitcast(U32).indirect(offs_t[:, lo // 16 : hi // 16]))
@@ -174,6 +181,7 @@ def tile_picked_gatv_none_p_kernel(
         grouped1 = [keep.tile([P, P, PACK], BF16, name=f"grouped1{b}", align_bytes=64) for b in range(BLOCKS)]
         for b in range(BLOCKS):
             cast(nc.scalar.copy, grouped1[b][:], late[b][:])
+        copy_row(2, AT_ROW2)
         words1 = [
             gather_words(keep.tile([P, hi - lo], U32, name=f"codes_x1_{lo}", align_bytes=64), window1, lo, hi)
             for lo, hi in pieces[:-1]
@@ -228,9 +236,8 @@ def tile_picked_gatv_none_p_kernel(
             nc.vector.tensor_tensor(product[:], picked, share_rows[d][:, lo:hi], ALU.mult)
             return product
 
-        def fetched(b, d):
-            columns = keep.tile([P, V], F32, name=f"columns{b}{d}")
-            nc.scalar.activation(columns[:], y[b][:].indirect(pos_t[d][:]), ACT.Copy)
+        def fetched(b, d, lo, hi, columns):
+            nc.scalar.activation(columns[:], y[b][:].indirect(pos_t[d][:, lo // 16 : hi // 16]), ACT.Copy)
             return columns
 
         product02 = [weighted(0, 2, 0, HALF)]
@@ -239,17 +246,17 @@ def tile_picked_gatv_none_p_kernel(
         product02.append(weighted(0, 2, HALF, V))
         turned = []
         for d in range(2):
-            columns = fetched(0, d)
+            columns = fetched(0, d, 0, V, keep.tile([P, V], F32, name=f"columns0{d}"))
             bank = psum.tile([P, CHUNKS, P], F32, name=f"turned{d}", tag=f"spare{d}")
             for c in range(CHUNKS):
                 nc.tensor.transpose(bank[:, c, :], columns[:, c * P : (c + 1) * P], ident[:])
             turned.append(bank)
-        columns12 = fetched(1, 2)
+        columns12 = [fetched(1, 2, 0, HALF, keep.tile([P, HALF], F32, name="columns12_0"))]
 
         back = [psum.tile([P, 2, P], F32, name=f"back{u}", tag=f"acc{u}_0") for u in range(2)]
         for u in range(2):
             for d in range(2):
-                scaled = keep.tile([P, 2, P], F32, name=f"scaled{u}{d}")
+                scaled = placed(f"scaled{u}{d}", [P, 2, P], F32, AT_SCALED + 8 * P * (2 * u + d))
                 for i in range(2):
                     c = 2 * u + i
                     nc.scalar.activation(
@@ -261,17 +268,17 @@ def tile_picked_gatv_none_p_kernel(
                         start=(d == 0 and i == 0), stop=(d == 1 and i == 1),
                     )
 
+        columns12.append(fetched(1, 2, HALF, V, placed("columns12_1", [P, HALF], F32, AT_SCALED)))
+
         halves = [slice(u * HALF, (u + 1) * HALF) for u in range(2)]
         part = keep.tile([P, V], F32, name="part")
-        for cols in halves:
-            nc.vector.tensor_tensor(part[:, cols], product10[:, cols], product11[:, cols], ALU.add)
-        product12 = keep.tile([P, V], F32, name="product12")
-        nc.vector.tensor_tensor(product12[:], columns12[:], share_rows[2], ALU.mult)
+        nc.vector.tensor_tensor(part[:], product10[:], product11[:], ALU.add)
         for u, cols in enumerate(halves):
-            result = keep.tile([P, HALF], F32, name=f"result1{u}")
-            nc.vector.tensor_tensor(result[:], part[:, cols], product12[:, cols], ALU.add)
-            nc.sync.dma_start(out[P:N, cols], result[:])
-        for u, cols in enumerate(halves):
+            product12 = keep.tile([P, HALF], F32, name=f"product12_{u}")
+            nc.vector.tensor_tensor(product12[:], columns12[u][:], share_rows[2][:, cols], ALU.mult)
             result = keep.tile([P, HALF], F32, name=f"result0{u}")
             nc.vector.tensor_tensor(result[:], back[u][:].rearrange("m i v -> m (i v)"), product02[u][:], ALU.add)
             nc.sync.dma_start(out[0:P, cols], result[:])
+            result = keep.tile([P, HALF], F32, name=f"result1{u}")
+            nc.vector.tensor_tensor(result[:], part[:, cols], product12[:], ALU.add)
+            nc.sync.dma_start(out[P:N, cols], result[:])

@@ -1,6 +1,7 @@
 from contextlib import ExitStack
 
 import concourse.mybir as mybir
+from concourse.masks import make_identity
 
 K, T, S, D, V, N = 1024, 2048, 1024, 3, 512, 256
 FLOPS = 2 * K * N * S
@@ -54,22 +55,13 @@ def tile_picked_gatv_none_p_kernel(
         pos_t = [lists.tile([P, V // 16], U16, name=f"pos_t{d}") for d in range(D)]
 
         scale_window = placed("scale_window", [P, T], U8, AT_SCALE_WINDOW)
-        nc.gpsimd.memset(scale_window[QUAD : 2 * QUAD, :].bitcast(I32), 0)
-        nc.gpsimd.memset(scale_window[2 * QUAD : P, :].bitcast(I32), 0)
+        nc.vector.memset(scale_window[QUAD : 2 * QUAD, :].bitcast(I32), 0)
+        nc.vector.memset(scale_window[2 * QUAD : P, :].bitcast(I32), 0)
 
         planes = keep.tile([P, S], U8, name="planes", align_bytes=64)
         nc.gpsimd.memset(planes[:].bitcast(I32), 0)
         ident = keep.tile([P, P], F32, name="ident")
-        nc.vector.memset(ident[:], 0.0)
-        ones = keep.tile([P, QUAD], F32, name="ones")
-        nc.vector.memset(ones[:], 1.0)
-        column = keep.tile([P, QUAD], F32, name="column", align_bytes=64)
-        nc.vector.tensor_tensor_scan(column[:], ones[:], ones[:], 0.0, ALU.mult, ALU.add)
-        row = keep.tile([P, QUAD], F32, name="row", align_bytes=64)
-        nc.vector.transpose(row[:], column[:])
-        for q in range(P // QUAD):
-            part = slice(QUAD * q, QUAD * (q + 1))
-            nc.vector.tensor_tensor(ident[part, part], column[part, :], row[part, :], ALU.is_equal)
+        make_identity(nc, ident[:])
 
         score_tile = keep.tile([P, D, 2 * PACK], F32, name="score_tile")
         scores = score_tile[:, :, 0:PACK]
@@ -216,11 +208,11 @@ def tile_picked_gatv_none_p_kernel(
                 multiply(1, b, i)
         for b in range(BLOCKS):
             multiply(1, b, len(pieces) - 1)
-        copy_out(nc.scalar.copy, 0, 0)
+        for b in range(BLOCKS):
+            copy_out(nc.scalar.copy, b, 0)
         for i in range(1, len(pieces)):
-            copy_out(nc.vector.tensor_copy, 0, i)
-        for i in range(len(pieces)):
-            copy_out(nc.scalar.copy, 1, i)
+            for b in range(BLOCKS):
+                copy_out(nc.vector.tensor_copy, b, i)
 
         share_columns = keep.tile([P, 2, CHUNKS], F32, name="share_columns")
         for d in range(2):

@@ -35,7 +35,6 @@ AT_LATE = 4 * V * 2 + 4 * V
 AT_SCALE_WINDOW = AT_LATE + QUARTER // 2
 AT_ROW2 = AT_LATE + 2 * QUARTER - 64
 AT_GROUPED0 = AT_ROW2 + 4 * V
-AT_SCALED = AT_GROUPED0 + 2 * PACK * N
 
 
 def tile_picked_gatv_none_p_kernel(
@@ -129,7 +128,9 @@ def tile_picked_gatv_none_p_kernel(
             nc.sync.dma_start(pos_t[d][:], pos)
 
         def cast(engine, grouped, rows):
-            engine(grouped, rows.rearrange("p j c -> p c j"))
+            engine(
+                grouped.rearrange("p (c i) j -> p c j i", i=PACK), rows.rearrange("p j (c i) -> p c j i", i=PACK)
+            )
 
         def quantize(name, grouped):
             width = grouped.shape[1]
@@ -178,9 +179,10 @@ def tile_picked_gatv_none_p_kernel(
             gather_words(keep.tile([P, hi - lo], U32, name=f"codes_x1_{lo}", align_bytes=64), window1, lo, hi)
             for lo, hi in pieces[:-1]
         ]
-        w_pass1 = quantize("w10", grouped1[0]) + quantize("w11", grouped1[1])
-        last = placed("codes_x1_last", [P, PIECE], U32, AT_LATE + QUARTER + QUARTER // 4)
+        w_pass1 = quantize("w10", grouped1[0])
+        last = placed("codes_x1_last", [P, PIECE], U32, AT_LATE)
         words1.append(gather_words(last, window1, *pieces[-1]))
+        w_pass1 = w_pass1 + quantize("w11", grouped1[1])
         y = [keep.tile([P, S], F32, name=f"y{b}") for b in range(BLOCKS)]
 
         def multiply(z, b, i):
@@ -204,73 +206,78 @@ def tile_picked_gatv_none_p_kernel(
             for i in range(len(pieces)):
                 multiply(0, b, i)
         for b in range(BLOCKS):
-            for i in range(len(pieces) - 1):
+            for i in range(len(pieces)):
                 multiply(1, b, i)
         for b in range(BLOCKS):
-            multiply(1, b, len(pieces) - 1)
-        for b in range(BLOCKS):
             copy_out(nc.scalar.copy, b, 0)
-        for i in range(1, len(pieces)):
-            for b in range(BLOCKS):
+        for b in range(BLOCKS):
+            for i in range(1, len(pieces)):
                 copy_out(nc.vector.tensor_copy, b, i)
 
-        share_columns = keep.tile([P, 2, CHUNKS], F32, name="share_columns")
-        for d in range(2):
-            bank = psum.tile([P, CHUNKS, P], F32, name=f"column{d}", tag=f"acc{d}_2")
-            for c in range(CHUNKS):
+        last_chunk = CHUNKS - 1
+        main = last_chunk * P
+        share_columns = keep.tile([P, D, CHUNKS], F32, name="share_columns")
+        for d in range(D):
+            chunks = range(CHUNKS) if d < 2 else [last_chunk]
+            bank = psum.tile([P, CHUNKS, P], F32, name=f"column{d}", tag=("acc0_2", "acc1_2", "acc0_1")[d])
+            for c in chunks:
                 nc.tensor.transpose(bank[:, c, :], share_rows[d][:, c * P : (c + 1) * P], ident[:])
-            nc.scalar.copy(share_columns[:, d, :], bank[:, :, 0])
+            nc.scalar.copy(share_columns[:, d, chunks[0] :], bank[:, chunks[0] :, 0])
 
-        def weighted(b, d, lo=0, hi=V):
-            name = f"product{b}{d}_{lo}"
-            product = placed(name, [P, hi - lo], F32, AT_ROWS) if lo else keep.tile([P, hi - lo], F32, name=name)
+        def weighted(b, d, lo, hi, product):
             picked = y[b][:].indirect(pos_t[d][:, lo // 16 : hi // 16])
             nc.vector.tensor_tensor(product[:], picked, share_rows[d][:, lo:hi], ALU.mult)
             return product
 
-        def fetched(b, d, lo, hi, columns):
+        def fetched(b, d, lo, hi):
+            columns = keep.tile([P, hi - lo], F32, name=f"columns{b}{d}")
             nc.scalar.activation(columns[:], y[b][:].indirect(pos_t[d][:, lo // 16 : hi // 16]), ACT.Copy)
             return columns
 
-        product02 = [weighted(0, 2, 0, HALF)]
-        product10 = weighted(1, 0)
-        product11 = weighted(1, 1)
-        product02.append(weighted(0, 2, HALF, V))
+        product02 = weighted(0, 2, 0, main, keep.tile([P, main], F32, name="product02"))
+        product10 = weighted(1, 0, 0, V, keep.tile([P, V], F32, name="product10"))
+        product11 = weighted(1, 1, 0, V, keep.tile([P, V], F32, name="product11"))
+        product12 = keep.tile([P, V], F32, name="product12")
+        weighted(1, 2, HALF, V, product12[:, HALF:V])
         turned = []
-        for d in range(2):
-            columns = fetched(0, d, 0, V, keep.tile([P, V], F32, name=f"columns0{d}"))
-            bank = psum.tile([P, CHUNKS, P], F32, name=f"turned{d}", tag=f"spare{d}")
-            for c in range(CHUNKS):
-                nc.tensor.transpose(bank[:, c, :], columns[:, c * P : (c + 1) * P], ident[:])
+        for d in range(D):
+            lo = 0 if d < 2 else main
+            columns = fetched(0, d, lo, V)
+            bank = psum.tile([P, CHUNKS, P], F32, name=f"turned{d}", tag=("spare0", "spare1", "acc1_1")[d])
+            for c in range(lo // P, CHUNKS):
+                nc.tensor.transpose(bank[:, c, :], columns[:, c * P - lo : (c + 1) * P - lo], ident[:])
             turned.append(bank)
-        columns12 = [fetched(1, 2, 0, HALF, keep.tile([P, HALF], F32, name="columns12_0"))]
+        columns12 = fetched(1, 2, 0, HALF)
 
-        back = [psum.tile([P, 2, P], F32, name=f"back{u}", tag=f"acc{u}_0") for u in range(2)]
-        for u in range(2):
-            for d in range(2):
-                scaled = placed(f"scaled{u}{d}", [P, 2, P], F32, AT_SCALED + 8 * P * (2 * u + d))
-                for i in range(2):
-                    c = 2 * u + i
+        def turn_back(name, tag, chunks, neighbours):
+            bank = psum.tile([P, len(chunks), P], F32, name=name, tag=tag)
+            for d in neighbours:
+                scaled = keep.tile([P, len(chunks), P], F32, name=f"scaled_{name}{d}")
+                for i, c in enumerate(chunks):
                     nc.scalar.activation(
                         scaled[:, i, :], turned[d][:, c, :], ACT.Copy, scale=share_columns[:, d, c : c + 1]
                     )
-                for i in range(2):
+                for i, c in enumerate(chunks):
                     nc.tensor.matmul(
-                        back[u][:, i, :], scaled[:, i, :], ident[:], is_transpose=True,
-                        start=(d == 0 and i == 0), stop=(d == 1 and i == 1),
+                        bank[:, i, :], scaled[:, i, :], ident[:], is_transpose=True,
+                        start=(d == neighbours[0] and i == 0), stop=(d == neighbours[-1] and i == len(chunks) - 1),
                     )
+            return bank[:].rearrange("m i v -> m (i v)")
 
-        columns12.append(fetched(1, 2, HALF, V, placed("columns12_1", [P, HALF], F32, AT_SCALED)))
+        back_main = turn_back("back_main", "acc0_0", range(last_chunk), range(2))
+        back_last = turn_back("back_last", "acc1_0", [last_chunk], range(D))
+        result = keep.tile([P, P], F32, name="result0_last")
+        nc.scalar.copy(result[:], back_last)
+        nc.sync.dma_start(out[0:P, main:V], result[:])
 
-        halves = [slice(u * HALF, (u + 1) * HALF) for u in range(2)]
         part = keep.tile([P, V], F32, name="part")
+        nc.vector.tensor_tensor(product12[:, 0:HALF], columns12[:], share_rows[2][:, 0:HALF], ALU.mult)
         nc.vector.tensor_tensor(part[:], product10[:], product11[:], ALU.add)
-        for u, cols in enumerate(halves):
-            product12 = keep.tile([P, HALF], F32, name=f"product12_{u}")
-            nc.vector.tensor_tensor(product12[:], columns12[u][:], share_rows[2][:, cols], ALU.mult)
-            result = keep.tile([P, HALF], F32, name=f"result0{u}")
-            nc.vector.tensor_tensor(result[:], back[u][:].rearrange("m i v -> m (i v)"), product02[u][:], ALU.add)
-            nc.sync.dma_start(out[0:P, cols], result[:])
+        result = keep.tile([P, main], F32, name="result0_main")
+        nc.vector.tensor_tensor(result[:], back_main, product02[:], ALU.add)
+        nc.sync.dma_start(out[0:P, 0:main], result[:])
+        for u in range(2):
+            cols = slice(u * HALF, (u + 1) * HALF)
             result = keep.tile([P, HALF], F32, name=f"result1{u}")
-            nc.vector.tensor_tensor(result[:], part[:, cols], product12[:], ALU.add)
+            nc.vector.tensor_tensor(result[:], part[:, cols], product12[:, cols], ALU.add)
             nc.sync.dma_start(out[P:N, cols], result[:])

@@ -27,6 +27,7 @@ HALF = V // 2
 BANK = 512
 PIECE = 256
 GAP = 12
+LEAD = 512
 
 QUARTER = 4 * PACK * P
 AT_ROWS = 0
@@ -62,6 +63,13 @@ def tile_picked_gatv_none_p_kernel(
         ident = keep.tile([P, P], F32, name="ident")
         make_identity(nc, ident[:])
 
+        def load_words(z, window, lo, hi):
+            words = x_words[z].rearrange("p c r -> p (c r)").bitcast(I32)
+            nc.sync.dma_start(window[:, lo:hi], words[:, lo:hi])
+
+        window0 = keep.tile([P, T], I32, name="window0", align_bytes=64)
+        window1 = keep.tile([P, T], I32, name="window1", align_bytes=64)
+        load_words(0, window0, 0, LEAD)
         score_tile = keep.tile([P, D, 2 * PACK], F32, name="score_tile")
         scores = score_tile[:, :, 0:PACK]
         nc.sync.dma_start(scores, score[:, 0, :].rearrange("d (p j) -> p d j", j=PACK))
@@ -70,19 +78,12 @@ def tile_picked_gatv_none_p_kernel(
             queue.dma_start(scale_window[first : first + hi - lo, :].bitcast(I32), x_scales[z, lo:hi, :].bitcast(I32))
         nc.sync.dma_start(offs_t[:], offs)
 
-        def load_words(z, cuts):
-            window = keep.tile([P, T], I32, name=f"window{z}", align_bytes=64)
-            words = x_words[z].rearrange("p c r -> p (c r)").bitcast(I32)
-            for lo, hi in zip(cuts, cuts[1:]):
-                nc.sync.dma_start(window[:, lo:hi], words[:, lo:hi])
-            return window
-
-        window0 = load_words(0, [0, T // 2, T])
+        load_words(0, window0, LEAD, T)
         raw0 = placed("raw0", [P, PACK, N], F32, AT_RAW0)
         nc.sync.dma_start(
             raw0[:].rearrange("p j c -> p (j c)"), w1[0 : P * PACK, :].rearrange("(p j) c -> p (j c)", j=PACK)
         )
-        window1 = load_words(1, [0, T])
+        load_words(1, window1, 0, T)
 
         neg_scores = keep.tile([P, D, PACK], F32, name="neg_scores")
         nc.scalar.activation(neg_scores[:], scores, ACT.Copy, scale=-1.0)

@@ -27,7 +27,7 @@ HALF = V // 2
 BANK = 512
 PIECE = 256
 GAP = 12
-LEAD = 512
+LEAD = 256
 
 QUARTER = 4 * PACK * P
 AT_ROWS = 0
@@ -176,10 +176,8 @@ def tile_picked_gatv_none_p_kernel(
         for b in range(BLOCKS):
             cast(nc.scalar.copy, grouped1[b][:], late[b][:])
         copy_row(2, AT_ROW2)
-        words1 = [
-            gather_words(keep.tile([P, hi - lo], U32, name=f"codes_x1_{lo}", align_bytes=64), window1, lo, hi)
-            for lo, hi in pieces[:-1]
-        ]
+        early = gather_words(keep.tile([P, S - PIECE], U32, name="codes_x1", align_bytes=64), window1, 0, S - PIECE)
+        words1 = [early[:, lo:hi] for lo, hi in pieces[:-1]]
         w_pass1 = quantize("w10", grouped1[0])
         last = placed("codes_x1_last", [P, PIECE], U32, AT_LATE)
         words1.append(gather_words(last, window1, *pieces[-1]))

@@ -25,17 +25,16 @@ BLOCKS = N // P
 CHUNKS = V // P
 HALF = V // 2
 BANK = 512
+BANK_BYTES = 4 * BANK
 PIECE = 256
 GAP = 12
 LEAD = 256
+ROW_STEP = 45
+FIRST_ROW = 12
+BASE = 96
 
-QUARTER = 4 * PACK * P
-AT_ROWS = 0
-AT_RAW0 = 2 * V
-AT_LATE = 4 * V * 2 + 4 * V
-AT_SCALE_WINDOW = AT_LATE + QUARTER // 2
-AT_ROW2 = AT_LATE + 2 * QUARTER - 64
-AT_GROUPED0 = AT_ROW2 + 4 * V
+AT_RAW0 = 0
+AT_LATE = 8 * BANK
 
 
 def tile_picked_gatv_none_p_kernel(
@@ -51,12 +50,14 @@ def tile_picked_gatv_none_p_kernel(
         def placed(name, shape, dtype, at):
             return reused.tile(shape, dtype, name=name, offset=at, align_bytes=64)
 
+        def in_bank(name, shape, bank):
+            return psum.tile(shape, F32, name=name, offset=bank * BANK_BYTES)
+
         offs_t = lists.tile([P, S // 16], U16, name="offs_t")
         pos_t = [lists.tile([P, V // 16], U16, name=f"pos_t{d}") for d in range(D)]
 
-        scale_window = placed("scale_window", [P, T], U8, AT_SCALE_WINDOW)
-        nc.vector.memset(scale_window[QUAD : 2 * QUAD, :].bitcast(I32), 0)
-        nc.vector.memset(scale_window[2 * QUAD : P, :].bitcast(I32), 0)
+        scale_window = placed("scale_window", [P, T], U8, AT_LATE + 2 * BANK)
+        nc.vector.memset(scale_window[0:BASE, :].bitcast(I32), 0)
 
         planes = keep.tile([P, S], U8, name="planes", align_bytes=64)
         nc.gpsimd.memset(planes[:].bitcast(I32), 0)
@@ -69,15 +70,16 @@ def tile_picked_gatv_none_p_kernel(
 
         window0 = keep.tile([P, T], I32, name="window0", align_bytes=64)
         window1 = keep.tile([P, T], I32, name="window1", align_bytes=64)
+        score_rows = keep.tile([P, QUAD], F32, name="score_rows", align_bytes=64)
+        nc.sync.dma_start(
+            score_rows[:],
+            score.rearrange("d r (c q i) -> q (d r c) i", q=4, i=QUAD)[:, 0 : QUAD * ROW_STEP : ROW_STEP, :],
+        )
         load_words(0, window0, 0, LEAD)
-        score_tile = keep.tile([P, D, 2 * PACK], F32, name="score_tile")
-        scores = score_tile[:, :, 0:PACK]
-        nc.sync.dma_start(scores, score[:, 0, :].rearrange("d (p j) -> p d j", j=PACK))
         scale_loads = ((nc.sync, 0, 0, 16, 0), (nc.sync, 1, 4, 12, 16), (nc.scalar, 1, 12, 16, 24), (nc.scalar, 1, 0, 4, 28))
         for queue, z, lo, hi, first in scale_loads:
-            queue.dma_start(scale_window[first : first + hi - lo, :].bitcast(I32), x_scales[z, lo:hi, :].bitcast(I32))
+            queue.dma_start(scale_window[BASE + first : BASE + first + hi - lo, :].bitcast(I32), x_scales[z, lo:hi, :].bitcast(I32))
         nc.sync.dma_start(offs_t[:], offs)
-
         load_words(0, window0, LEAD, T)
         raw0 = placed("raw0", [P, PACK, N], F32, AT_RAW0)
         nc.sync.dma_start(
@@ -85,81 +87,70 @@ def tile_picked_gatv_none_p_kernel(
         )
         load_words(1, window1, 0, T)
 
-        neg_scores = keep.tile([P, D, PACK], F32, name="neg_scores")
+        turned_scores = keep.tile([P, D * FIRST_ROW], F32, name="turned_scores", align_bytes=64)
+        nc.vector.transpose(turned_scores[:, 0:QUAD], score_rows[:])
+        scores = turned_scores[:].rearrange("p (d c) -> p c d", c=FIRST_ROW)[:, 0:CHUNKS, :]
+        neg_scores = keep.tile([P, CHUNKS, D], F32, name="neg_scores")
         nc.scalar.activation(neg_scores[:], scores, ACT.Copy, scale=-1.0)
-        neg_top = keep.tile([P, PACK], F32, name="neg_top")
-        nc.vector.tensor_reduce(
-            neg_top[:], scores.rearrange("p d j -> p j d"), mybir.AxisListType.X, ALU.max, negate=True
-        )
-        exps = placed("exps", [P, D, PACK], F32, AT_GROUPED0)
-        total = keep.tile([P, PACK], F32, name="total")
-        for j in range(PACK):
+        neg_top = keep.tile([P, CHUNKS], F32, name="neg_top")
+        nc.vector.tensor_reduce(neg_top[:], scores, mybir.AxisListType.X, ALU.max, negate=True)
+        exps = keep.tile([P, D, CHUNKS], F32, name="exps")
+        total = keep.tile([P, CHUNKS], F32, name="total")
+        for c in range(CHUNKS):
             nc.scalar.activation(
-                exps[:, :, j], neg_scores[:, :, j], ACT.Exp, scale=-1.0, bias=neg_top[:, j : j + 1],
-                accum_out=total[:, j : j + 1],
+                exps[:, :, c], neg_scores[:, c, :], ACT.Exp, scale=-1.0, bias=neg_top[:, c : c + 1],
+                accum_out=total[:, c : c + 1],
             )
 
-        scales_x = keep.tile([P, S], U8, name="scales_x", align_bytes=64)
-        nc.vector.tensor_copy(scales_x[:], scale_window[:].indirect(offs_t[:]))
+        def by_fours(grouped, rows):
+            return grouped.rearrange("p (c i) j -> p c j i", i=PACK), rows.rearrange("p j (c i) -> p c j i", i=PACK)
 
-        def move_rows(queue, to, first, count):
-            queue.dma_start(planes[to : to + count, :].bitcast(I32), scales_x[first : first + count, :].bitcast(I32))
-
-        for q in range(1, 4):
-            move_rows(nc.sync, QUAD * q, 4 * q, GAP + 4)
-        move_rows(nc.sync, 0, 0, 4)
-        move_rows(nc.sync, GAP, 28, 4)
-
-        root = keep.tile([P, PACK], F32, name="root")
-        nc.scalar.activation(root[:], total[:], ACT.Abs_reciprocal_sqrt)
-        inverse = keep.tile([P, PACK], F32, name="inverse")
-        nc.scalar.activation(inverse[:], root[:], ACT.Square)
-        shares = keep.tile([P, D, PACK], F32, name="shares")
-        for j in range(PACK):
-            nc.scalar.activation(shares[:, :, j], exps[:, :, j], ACT.Copy, scale=inverse[:, j : j + 1])
-
-        late = []
-        for b in range(BLOCKS):
-            late.append(placed(f"late{b}", [P, PACK, P], F32, AT_LATE + QUARTER * b))
-            nc.sync.dma_start(
-                late[b][:], w1[P * PACK : K, b * P : (b + 1) * P].rearrange("(p j) c -> p j c", j=PACK)
-            )
-
-        for d, pos in enumerate((pos1, pos2, pos3)):
-            nc.sync.dma_start(pos_t[d][:], pos)
-
-        def cast(engine, grouped, rows):
-            engine(
-                grouped.rearrange("p (c i) j -> p c j i", i=PACK), rows.rearrange("p j (c i) -> p c j i", i=PACK)
-            )
-
-        def quantize(name, grouped):
+        def quantize(codes, name, grouped):
             width = grouped.shape[1]
-            codes = keep.tile([P, width], U32, name=f"codes_{name}", align_bytes=64)
             scales = keep.tile([P, width], U8, name=f"scales_{name}", align_bytes=64)
             nc.vector.quantize_mx(
                 out=codes[:].bitcast(FP8X4), scales=scales[:], in_=grouped[:].rearrange("p c j -> p (c j)")
             )
             return [(codes[:, c : c + P], scales[:, c : c + P]) for c in range(0, width, P)]
 
-        grouped0 = placed("grouped0", [P, N, PACK], BF16, AT_GROUPED0)
-        cast(nc.scalar.copy, grouped0[:], raw0[:])
 
+        scales_x = keep.tile([P, S], U8, name="scales_x", align_bytes=64)
+        nc.vector.tensor_copy(scales_x[:], scale_window[:].indirect(offs_t[:]))
+        inverse = keep.tile([P, CHUNKS], F32, name="inverse")
+        nc.vector.reciprocal(inverse[:], total[:])
+        shares = keep.tile([P, D, CHUNKS], F32, name="shares")
+        for c in range(CHUNKS):
+            nc.scalar.activation(shares[:, :, c], exps[:, :, c], ACT.Copy, scale=inverse[:, c : c + 1])
+
+        def move_rows(to, first, count):
+            nc.sync.dma_start(planes[to : to + count, :].bitcast(I32), scales_x[BASE + first : BASE + first + count, :].bitcast(I32))
+
+        for q in range(1, 4):
+            move_rows(QUAD * q, 4 * q, GAP + 4)
+        move_rows(0, 0, 4)
+        move_rows(GAP, 28, 4)
+
+        late = []
+        for b in range(BLOCKS):
+            late.append(placed(f"late{b}", [P, PACK, P], F32, AT_LATE + 4 * BANK * b))
+            nc.sync.dma_start(
+                late[b][:], w1[P * PACK : K, b * P : (b + 1) * P].rearrange("(p j) c -> p j c", j=PACK)
+            )
+        for d, pos in enumerate((pos1, pos2, pos3)):
+            nc.sync.dma_start(pos_t[d][:], pos)
+
+
+        grouped0 = keep.tile([P, N, PACK], BF16, name="grouped0", align_bytes=64)
+        nc.scalar.copy(*by_fours(grouped0[:], raw0[:]))
         spreads = []
         for d in range(D):
-            bank = psum.tile([P, PACK, P], F32, name=f"spread{d}", tag=("acc1_2", "spare0", "spare1")[d])
-            for j in range(PACK):
-                nc.tensor.transpose(bank[:, j, :], shares[:, d, j : j + 1].to_broadcast([P, P]), ident[:])
-            spreads.append(bank)
-        share_rows = []
-
-        def copy_row(d, at):
-            tile = placed(f"share_row{d}", [P, P, PACK], F32, at)
-            nc.scalar.copy(tile[:], spreads[d][:].rearrange("m j p -> m p j"))
-            share_rows.append(tile[:].rearrange("m p j -> m (p j)"))
-
-        for d in range(2):
-            copy_row(d, AT_ROWS + 4 * V * d)
+            bank = in_bank(f"spread{d}", [P, CHUNKS, P], (5, 6, 7)[d])
+            for c in range(CHUNKS):
+                nc.tensor.transpose(bank[:, c, :], shares[:, d, c : c + 1].to_broadcast([P, P]), ident[:])
+            spreads.append(bank[:].rearrange("m c p -> m (c p)"))
+        share_rows = [keep.tile([P, V], F32, name=f"share_row{d}") for d in range(D - 1)]
+        for d in range(D - 1):
+            nc.scalar.copy(share_rows[d][:], spreads[d])
 
         def gather_words(piece, window, lo, hi):
             nc.vector.tensor_copy(piece[:], window[:].bitcast(U32).indirect(offs_t[:, lo // 16 : hi // 16]))
@@ -167,21 +158,23 @@ def tile_picked_gatv_none_p_kernel(
 
         pieces = [(0, BANK), (BANK, S - PIECE), (S - PIECE, S)]
         acc = [
-            [psum.tile([P, hi - lo], F32, name=f"acc{b}_{i}", tag=f"acc{b}_{i}") for i, (lo, hi) in enumerate(pieces)]
-            for b in range(BLOCKS)
+            [in_bank(f"acc{b}_{i}", [P, hi - lo], 2 * i + b) for i, (lo, hi) in enumerate(pieces)] for b in range(BLOCKS)
         ]
-        codes_x0 = gather_words(keep.tile([P, S], U32, name="codes_x0", align_bytes=64), window0, 0, S)
-        w_pass0 = quantize("w0", grouped0)
+        front0 = gather_words(keep.tile([P, BANK], U32, name="codes_x0_front", align_bytes=64), window0, 0, BANK)
+        back0 = gather_words(keep.tile([P, BANK], U32, name="codes_x0_back", align_bytes=64), window0, BANK, S)
+        w_pass0 = quantize(keep.tile([P, N], U32, name="codes_w0", align_bytes=64), "w0", grouped0)
+        words0 = [front0, back0[:, 0:PIECE], back0[:, PIECE:BANK]]
         grouped1 = [keep.tile([P, P, PACK], BF16, name=f"grouped1{b}", align_bytes=64) for b in range(BLOCKS)]
         for b in range(BLOCKS):
-            cast(nc.scalar.copy, grouped1[b][:], late[b][:])
-        copy_row(2, AT_ROW2)
+            nc.scalar.copy(*by_fours(grouped1[b][:], late[b][:]))
+        share_rows.append(placed("share_row2", [P, V], F32, AT_LATE + 6 * BANK))
+        nc.scalar.copy(share_rows[2][:], spreads[2])
         early = gather_words(keep.tile([P, S - PIECE], U32, name="codes_x1", align_bytes=64), window1, 0, S - PIECE)
         words1 = [early[:, lo:hi] for lo, hi in pieces[:-1]]
-        w_pass1 = quantize("w10", grouped1[0])
+        w_pass1 = quantize(keep.tile([P, P], U32, name="codes_w10", align_bytes=64), "w10", grouped1[0])
         last = placed("codes_x1_last", [P, PIECE], U32, AT_LATE)
         words1.append(gather_words(last, window1, *pieces[-1]))
-        w_pass1 = w_pass1 + quantize("w11", grouped1[1])
+        w_pass1 = w_pass1 + quantize(keep.tile([P, P], U32, name="codes_w11", align_bytes=64), "w11", grouped1[1])
         y = [keep.tile([P, S], F32, name=f"y{b}") for b in range(BLOCKS)]
 
         def multiply(z, b, i):
@@ -191,7 +184,7 @@ def tile_picked_gatv_none_p_kernel(
                 out=acc[b][i][:],
                 lhsT=codes.bitcast(FP8X4),
                 lhsT_scale=scales,
-                rhs=(codes_x0[:, lo:hi] if z == 0 else words1[i]).bitcast(FP8X4),
+                rhs=(words0, words1)[z][i].bitcast(FP8X4),
                 rhs_scale=planes[GAP * z : P, lo:hi],
                 start=(z == 0),
                 stop=(z == PASSES - 1),
@@ -201,8 +194,8 @@ def tile_picked_gatv_none_p_kernel(
             lo, hi = pieces[i]
             engine(y[b][:, lo:hi], acc[b][i][:])
 
-        for b in range(BLOCKS):
-            for i in range(len(pieces)):
+        for i in range(len(pieces)):
+            for b in range(BLOCKS):
                 multiply(0, b, i)
         for b in range(BLOCKS):
             for i in range(len(pieces)):
@@ -215,13 +208,6 @@ def tile_picked_gatv_none_p_kernel(
 
         last_chunk = CHUNKS - 1
         main = last_chunk * P
-        share_columns = keep.tile([P, D, CHUNKS], F32, name="share_columns")
-        for d in range(D):
-            chunks = range(CHUNKS) if d < 2 else [last_chunk]
-            bank = psum.tile([P, CHUNKS, P], F32, name=f"column{d}", tag=("acc0_2", "acc1_2", "acc0_1")[d])
-            for c in chunks:
-                nc.tensor.transpose(bank[:, c, :], share_rows[d][:, c * P : (c + 1) * P], ident[:])
-            nc.scalar.copy(share_columns[:, d, chunks[0] :], bank[:, chunks[0] :, 0])
 
         def weighted(b, d, lo, hi, product):
             picked = y[b][:].indirect(pos_t[d][:, lo // 16 : hi // 16])
@@ -242,19 +228,19 @@ def tile_picked_gatv_none_p_kernel(
         for d in range(D):
             lo = 0 if d < 2 else main
             columns = fetched(0, d, lo, V)
-            bank = psum.tile([P, CHUNKS, P], F32, name=f"turned{d}", tag=("spare0", "spare1", "acc1_1")[d])
+            bank = in_bank(f"turned{d}", [P, CHUNKS, P], (6, 7, 3)[d])
             for c in range(lo // P, CHUNKS):
                 nc.tensor.transpose(bank[:, c, :], columns[:, c * P - lo : (c + 1) * P - lo], ident[:])
             turned.append(bank)
         columns12 = fetched(1, 2, 0, HALF)
 
-        def turn_back(name, tag, chunks, neighbours):
-            bank = psum.tile([P, len(chunks), P], F32, name=name, tag=tag)
+        def turn_back(name, at, chunks, neighbours):
+            bank = in_bank(name, [P, len(chunks), P], at)
             for d in neighbours:
                 scaled = keep.tile([P, len(chunks), P], F32, name=f"scaled_{name}{d}")
                 for i, c in enumerate(chunks):
                     nc.scalar.activation(
-                        scaled[:, i, :], turned[d][:, c, :], ACT.Copy, scale=share_columns[:, d, c : c + 1]
+                        scaled[:, i, :], turned[d][:, c, :], ACT.Copy, scale=shares[:, d, c : c + 1]
                     )
                 for i, c in enumerate(chunks):
                     nc.tensor.matmul(
@@ -263,8 +249,8 @@ def tile_picked_gatv_none_p_kernel(
                     )
             return bank[:].rearrange("m i v -> m (i v)")
 
-        back_main = turn_back("back_main", "acc0_0", range(last_chunk), range(2))
-        back_last = turn_back("back_last", "acc1_0", [last_chunk], range(D))
+        back_main = turn_back("back_main", 0, range(last_chunk), range(2))
+        back_last = turn_back("back_last", 1, [last_chunk], range(D))
         result = keep.tile([P, P], F32, name="result0_last")
         nc.scalar.copy(result[:], back_last)
         nc.sync.dma_start(out[0:P, main:V], result[:])

from contextlib import ExitStack

import concourse.mybir as mybir
from concourse.masks import make_identity

K, T, S, D, V, N = 1024, 2048, 1024, 3, 512, 256
FLOPS = 2 * K * N * S
BYTES = K * T + K * T // 32 + K * N * 4 + D * V * 4 + 128 * (S + D * V) // 16 * 2 + N * V * 4

F32 = mybir.dt.float32
BF16 = mybir.dt.bfloat16
I32 = mybir.dt.int32
U32 = mybir.dt.uint32
U16 = mybir.dt.uint16
U8 = mybir.dt.uint8
FP8X4 = mybir.dt.float8_e4m3fn_x4
ALU = mybir.AluOpType
ACT = mybir.ActivationFunctionType

P = 128
QUAD = 32
PACK = 4
PASSES = K // (P * PACK)
BLOCKS = N // P
CHUNKS = V // P
HALF = V // 2
BANK = 512
BANK_BYTES = 4 * BANK
PIECE = 256
GAP = 12
LEAD = 256
ROW_STEP = 45
FIRST_ROW = 12
BASE = 96

AT_RAW0 = 0
AT_LATE = 8 * BANK


def tile_picked_gatv_none_p_kernel(
    tc, x_words, x_scales, w1, score, offs, pos1, pos2, pos3, out
):
    nc = tc.nc
    with ExitStack() as ctx:
        lists = ctx.enter_context(tc.tile_pool(name="lists", bufs=1))
        keep = ctx.enter_context(tc.tile_pool(name="keep", bufs=1))
        reused = ctx.enter_context(tc.tile_pool(name="reused", bufs=1))
        psum = ctx.enter_context(tc.psum_pool(name="psum", bufs=1))

        def placed(name, shape, dtype, at):
            return reused.tile(shape, dtype, name=name, offset=at, align_bytes=64)

        def in_bank(name, shape, bank):
            return psum.tile(shape, F32, name=name, offset=bank * BANK_BYTES)

        offs_t = lists.tile([P, S // 16], U16, name="offs_t")
        pos_t = [lists.tile([P, V // 16], U16, name=f"pos_t{d}") for d in range(D)]

        scale_window = placed("scale_window", [P, T], U8, AT_LATE + 2 * BANK)
        nc.vector.memset(scale_window[0:BASE, :].bitcast(I32), 0)

        planes = keep.tile([P, S], U8, name="planes", align_bytes=64)
        nc.gpsimd.memset(planes[:].bitcast(I32), 0)
        ident = keep.tile([P, P], F32, name="ident")
        make_identity(nc, ident[:])

        def load_words(z, window, lo, hi):
            words = x_words[z].rearrange("p c r -> p (c r)").bitcast(I32)
            nc.sync.dma_start(window[:, lo:hi], words[:, lo:hi])

        window0 = keep.tile([P, T], I32, name="window0", align_bytes=64)
        window1 = keep.tile([P, T], I32, name="window1", align_bytes=64)
        score_rows = keep.tile([P, QUAD], F32, name="score_rows", align_bytes=64)
        nc.sync.dma_start(
            score_rows[:],
            score.rearrange("d r (c q i) -> q (d r c) i", q=4, i=QUAD)[:, 0 : QUAD * ROW_STEP : ROW_STEP, :],
        )
        load_words(0, window0, 0, LEAD)
        scale_loads = ((nc.sync, 0, 0, 16, 0), (nc.sync, 1, 4, 12, 16), (nc.scalar, 1, 12, 16, 24), (nc.scalar, 1, 0, 4, 28))
        for queue, z, lo, hi, first in scale_loads:
            queue.dma_start(scale_window[BASE + first : BASE + first + hi - lo, :].bitcast(I32), x_scales[z, lo:hi, :].bitcast(I32))
        nc.sync.dma_start(offs_t[:], offs)
        load_words(0, window0, LEAD, T)
        raw0 = placed("raw0", [P, PACK, N], F32, AT_RAW0)
        nc.sync.dma_start(
            raw0[:].rearrange("p j c -> p (j c)"), w1[0 : P * PACK, :].rearrange("(p j) c -> p (j c)", j=PACK)
        )
        load_words(1, window1, 0, T)

        turned_scores = keep.tile([P, D * FIRST_ROW], F32, name="turned_scores", align_bytes=64)
        nc.vector.transpose(turned_scores[:, 0:QUAD], score_rows[:])
        scores = turned_scores[:].rearrange("p (d c) -> p c d", c=FIRST_ROW)[:, 0:CHUNKS, :]
        neg_scores = keep.tile([P, CHUNKS, D], F32, name="neg_scores")
        nc.scalar.activation(neg_scores[:], scores, ACT.Copy, scale=-1.0)
        neg_top = keep.tile([P, CHUNKS], F32, name="neg_top")
        nc.vector.tensor_reduce(neg_top[:], scores, mybir.AxisListType.X, ALU.max, negate=True)
        exps = keep.tile([P, D, CHUNKS], F32, name="exps")
        total = keep.tile([P, CHUNKS], F32, name="total")
        for c in range(CHUNKS):
            nc.scalar.activation(
                exps[:, :, c], neg_scores[:, c, :], ACT.Exp, scale=-1.0, bias=neg_top[:, c : c + 1],
                accum_out=total[:, c : c + 1],
            )

        def by_fours(grouped, rows):
            return grouped.rearrange("p (c i) j -> p c j i", i=PACK), rows.rearrange("p j (c i) -> p c j i", i=PACK)

        def quantize(codes, name, grouped):
            width = grouped.shape[1]
            scales = keep.tile([P, width], U8, name=f"scales_{name}", align_bytes=64)
            nc.vector.quantize_mx(
                out=codes[:].bitcast(FP8X4), scales=scales[:], in_=grouped[:].rearrange("p c j -> p (c j)")
            )
            return [(codes[:, c : c + P], scales[:, c : c + P]) for c in range(0, width, P)]


        scales_x = keep.tile([P, S], U8, name="scales_x", align_bytes=64)
        nc.vector.tensor_copy(scales_x[:], scale_window[:].indirect(offs_t[:]))
        inverse = keep.tile([P, CHUNKS], F32, name="inverse")
        nc.vector.reciprocal(inverse[:], total[:])
        shares = keep.tile([P, D, CHUNKS], F32, name="shares")
        for c in range(CHUNKS):
            nc.scalar.activation(shares[:, :, c], exps[:, :, c], ACT.Copy, scale=inverse[:, c : c + 1])

        def move_rows(to, first, count):
            nc.sync.dma_start(planes[to : to + count, :].bitcast(I32), scales_x[BASE + first : BASE + first + count, :].bitcast(I32))

        for q in range(1, 4):
            move_rows(QUAD * q, 4 * q, GAP + 4)
        move_rows(0, 0, 4)
        move_rows(GAP, 28, 4)

        late = []
        for b in range(BLOCKS):
            late.append(placed(f"late{b}", [P, PACK, P], F32, AT_LATE + 4 * BANK * b))
            nc.sync.dma_start(
                late[b][:], w1[P * PACK : K, b * P : (b + 1) * P].rearrange("(p j) c -> p j c", j=PACK)
            )
        for d, pos in enumerate((pos1, pos2, pos3)):
            nc.sync.dma_start(pos_t[d][:], pos)


        grouped0 = keep.tile([P, N, PACK], BF16, name="grouped0", align_bytes=64)
        nc.scalar.copy(*by_fours(grouped0[:], raw0[:]))
        spreads = []
        for d in range(D):
            bank = in_bank(f"spread{d}", [P, CHUNKS, P], (5, 6, 7)[d])
            for c in range(CHUNKS):
                nc.tensor.transpose(bank[:, c, :], shares[:, d, c : c + 1].to_broadcast([P, P]), ident[:])
            spreads.append(bank[:].rearrange("m c p -> m (c p)"))
        share_rows = [keep.tile([P, V], F32, name=f"share_row{d}") for d in range(D - 1)]
        for d in range(D - 1):
            nc.scalar.copy(share_rows[d][:], spreads[d])

        def gather_words(piece, window, lo, hi):
            nc.vector.tensor_copy(piece[:], window[:].bitcast(U32).indirect(offs_t[:, lo // 16 : hi // 16]))
            return piece[:]

        pieces = [(0, BANK), (BANK, S - PIECE), (S - PIECE, S)]
        acc = [
            [in_bank(f"acc{b}_{i}", [P, hi - lo], 2 * i + b) for i, (lo, hi) in enumerate(pieces)] for b in range(BLOCKS)
        ]
        front0 = gather_words(keep.tile([P, BANK], U32, name="codes_x0_front", align_bytes=64), window0, 0, BANK)
        back0 = gather_words(keep.tile([P, BANK], U32, name="codes_x0_back", align_bytes=64), window0, BANK, S)
        w_pass0 = quantize(keep.tile([P, N], U32, name="codes_w0", align_bytes=64), "w0", grouped0)
        words0 = [front0, back0[:, 0:PIECE], back0[:, PIECE:BANK]]
        grouped1 = [keep.tile([P, P, PACK], BF16, name=f"grouped1{b}", align_bytes=64) for b in range(BLOCKS)]
        for b in range(BLOCKS):
            nc.scalar.copy(*by_fours(grouped1[b][:], late[b][:]))
        share_rows.append(placed("share_row2", [P, V], F32, AT_LATE + 6 * BANK))
        nc.scalar.copy(share_rows[2][:], spreads[2])
        early = gather_words(keep.tile([P, S - PIECE], U32, name="codes_x1", align_bytes=64), window1, 0, S - PIECE)
        words1 = [early[:, lo:hi] for lo, hi in pieces[:-1]]
        w_pass1 = quantize(keep.tile([P, P], U32, name="codes_w10", align_bytes=64), "w10", grouped1[0])
        last = placed("codes_x1_last", [P, PIECE], U32, AT_LATE)
        words1.append(gather_words(last, window1, *pieces[-1]))
        w_pass1 = w_pass1 + quantize(keep.tile([P, P], U32, name="codes_w11", align_bytes=64), "w11", grouped1[1])
        y = [keep.tile([P, S], F32, name=f"y{b}") for b in range(BLOCKS)]

        def multiply(z, b, i):
            lo, hi = pieces[i]
            codes, scales = (w_pass0, w_pass1)[z][b]
            nc.tensor.matmul_mx(
                out=acc[b][i][:],
                lhsT=codes.bitcast(FP8X4),
                lhsT_scale=scales,
                rhs=(words0, words1)[z][i].bitcast(FP8X4),
                rhs_scale=planes[GAP * z : P, lo:hi],
                start=(z == 0),
                stop=(z == PASSES - 1),
            )

        def copy_out(engine, b, i):
            lo, hi = pieces[i]
            engine(y[b][:, lo:hi], acc[b][i][:])

        for i in range(len(pieces)):
            for b in range(BLOCKS):
                multiply(0, b, i)
        for b in range(BLOCKS):
            for i in range(len(pieces)):
                multiply(1, b, i)
        for b in range(BLOCKS):
            copy_out(nc.scalar.copy, b, 0)
        for b in range(BLOCKS):
            for i in range(1, len(pieces)):
                copy_out(nc.vector.tensor_copy, b, i)

        last_chunk = CHUNKS - 1
        main = last_chunk * P

        def weighted(b, d, lo, hi, product):
            picked = y[b][:].indirect(pos_t[d][:, lo // 16 : hi // 16])
            nc.vector.tensor_tensor(product[:], picked, share_rows[d][:, lo:hi], ALU.mult)
            return product

        def fetched(b, d, lo, hi):
            columns = keep.tile([P, hi - lo], F32, name=f"columns{b}{d}")
            nc.scalar.activation(columns[:], y[b][:].indirect(pos_t[d][:, lo // 16 : hi // 16]), ACT.Copy)
            return columns

        product02 = weighted(0, 2, 0, main, keep.tile([P, main], F32, name="product02"))
        product10 = weighted(1, 0, 0, V, keep.tile([P, V], F32, name="product10"))
        product11 = weighted(1, 1, 0, V, keep.tile([P, V], F32, name="product11"))
        product12 = keep.tile([P, V], F32, name="product12")
        weighted(1, 2, HALF, V, product12[:, HALF:V])
        turned = []
        for d in range(D):
            lo = 0 if d < 2 else main
            columns = fetched(0, d, lo, V)
            bank = in_bank(f"turned{d}", [P, CHUNKS, P], (6, 7, 3)[d])
            for c in range(lo // P, CHUNKS):
                nc.tensor.transpose(bank[:, c, :], columns[:, c * P - lo : (c + 1) * P - lo], ident[:])
            turned.append(bank)
        columns12 = fetched(1, 2, 0, HALF)

        def turn_back(name, at, chunks, neighbours):
            bank = in_bank(name, [P, len(chunks), P], at)
            for d in neighbours:
                scaled = keep.tile([P, len(chunks), P], F32, name=f"scaled_{name}{d}")
                for i, c in enumerate(chunks):
                    nc.scalar.activation(
                        scaled[:, i, :], turned[d][:, c, :], ACT.Copy, scale=shares[:, d, c : c + 1]
                    )
                for i, c in enumerate(chunks):
                    nc.tensor.matmul(
                        bank[:, i, :], scaled[:, i, :], ident[:], is_transpose=True,
                        start=(d == neighbours[0] and i == 0), stop=(d == neighbours[-1] and i == len(chunks) - 1),
                    )
            return bank[:].rearrange("m i v -> m (i v)")

        back_main = turn_back("back_main", 0, range(last_chunk), range(2))
        back_last = turn_back("back_last", 1, [last_chunk], range(D))
        result = keep.tile([P, P], F32, name="result0_last")
        nc.scalar.copy(result[:], back_last)
        nc.sync.dma_start(out[0:P, main:V], result[:])

        part = keep.tile([P, V], F32, name="part")
        nc.vector.tensor_tensor(product12[:, 0:HALF], columns12[:], share_rows[2][:, 0:HALF], ALU.mult)
        nc.vector.tensor_tensor(part[:], product10[:], product11[:], ALU.add)
        result = keep.tile([P, main], F32, name="result0_main")
        nc.vector.tensor_tensor(result[:], back_main, product02[:], ALU.add)
        nc.sync.dma_start(out[0:P, 0:main], result[:])
        for u in range(2):
            cols = slice(u * HALF, (u + 1) * HALF)
            result = keep.tile([P, HALF], F32, name=f"result1{u}")
            nc.vector.tensor_tensor(result[:], part[:, cols], product12[:, cols], ALU.add)
            nc.sync.dma_start(out[P:N, cols], result[:])
